import numpy as np
import ml_dtypes


def mxq(x, axis, fmt="e4m3"):
    dtype, down = {"e4m3": (ml_dtypes.float8_e4m3fn, 7), "e5m2": (ml_dtypes.float8_e5m2, 14)}[fmt]
    v = np.moveaxis(np.asarray(x, np.float32).astype(ml_dtypes.bfloat16).astype(np.float64), axis, -1)
    blocks = v.reshape(v.shape[:-1] + (-1, 32))
    amax = np.abs(blocks).max(-1, keepdims=True)
    byte = np.maximum(np.where(amax > 0, np.frexp(amax)[1] - 1 + 127, 0) - down, 1)
    scale = np.exp2(byte - 127.0)
    codes = (blocks / scale).astype(np.float32).astype(dtype).astype(np.float64)
    return np.moveaxis((codes * scale).reshape(v.shape), -1, axis)


WIDE = False


def mx_kscale(k):
    if not WIDE:
        return np.ones(k)
    levels = np.array([10, -10, 5, -5, 0])
    if k % 512:
        return np.exp2(np.random.permutation(np.resize(levels, k // 32))).repeat(32)
    a = np.empty((k // 512, 16))
    for p in range(k // 512):
        a[p, :8] = np.random.permutation(np.resize(levels, 8))
        for g in range(8):
            far = levels[np.abs(levels - a[p, g]) >= 10]
            a[p, g + 8] = far[np.random.randint(len(far))]
    return np.exp2(a.ravel()).repeat(32)


def f64(x):
    return np.asarray(x).astype(np.float64)


def striped(idx):
    return np.tile(idx.reshape(-1, 16).T, (8, 1)).astype(np.uint16)


def unstriped(offs):
    return offs[:16].T.reshape(-1).astype(np.int64)


E2M1 = np.array([0.0, 0.5, 1.0, 1.5, 2.0, 3.0, 4.0, 6.0, -0.0, -0.5, -1.0, -1.5, -2.0, -3.0, -4.0, -6.0])


def pack_weight(w, fmt):
    k, n = w.shape
    w = f64(np.asarray(w, np.float32).astype(ml_dtypes.bfloat16)).reshape(k // 32, 32, n)
    amax = np.abs(w).max(1)
    if fmt == "e4m3":
        byte = np.frexp(amax)[1] - 1 + 127 - 7
    else:
        mant, ex = np.frexp(amax / 6.0)
        byte = np.where(mant > 0.5, ex, ex - 1) + 127
    byte = np.clip(np.where(amax > 0, byte, 1), 1, 254)
    scaled = (w * np.exp2(127.0 - byte)[:, None, :]).reshape(k, n).astype(np.float32)
    by_word = np.ascontiguousarray(scaled.reshape(k // 512, 128, 4, n).transpose(0, 1, 3, 2))
    if fmt == "e4m3":
        words = by_word.astype(ml_dtypes.float8_e4m3fn).view(np.uint8)
    else:
        c = by_word.astype(ml_dtypes.float4_e2m1fn).view(np.uint8) & 0xF
        words = (c[..., 0::2] | (c[..., 1::2] << 4)).reshape(k // 512, 128, 2 * n)
    return np.ascontiguousarray(words), np.ascontiguousarray(byte.astype(np.uint8).reshape(k // 512, 16, n))


def unpack_weight(words, scales, fmt):
    g, _, n = scales.shape
    words = np.ascontiguousarray(words).reshape(g, 128, n, -1)
    if fmt == "e4m3":
        vals = words.view(ml_dtypes.float8_e4m3fn).astype(np.float64)
    else:
        nib = np.empty((g, 128, n, 4), np.uint8)
        nib[..., 0::2] = words & 0xF
        nib[..., 1::2] = words >> 4
        vals = E2M1[nib]
    vals = vals * np.repeat(np.exp2(scales.astype(np.float64) - 127.0), 8, axis=1)[..., None]
    return vals.transpose(0, 1, 3, 2).reshape(g * 512, n)


def gelu(v):
    return 0.5 * v * (1.0 + np.tanh(np.sqrt(2.0 / np.pi) * (v + 0.044715 * v**3)))


def striped8(idx):
    return np.concatenate([v.reshape(-1, 16).T for v in idx]).astype(np.uint16)


def unstriped8(offs):
    return np.stack([offs[16 * g:16 * g + 16].T.reshape(-1) for g in range(8)]).astype(np.int64)


def put_heads(h, wgs, idx8, t2):
    r = np.arange(h.shape[0])
    page = np.zeros((h.shape[0], t2))
    page[r[:, None], idx8[r % 512 // 64]] = wgs[r // 4 % 128] * h
    return page


def bf(x):
    return np.asarray(x, np.float32).astype(ml_dtypes.bfloat16)


def planes(Y):
    n, m = Y.shape
    b = f64(bf(Y)).reshape(n // 32, 32, m)
    amax = np.abs(b).max(1)
    byte = np.clip(np.where(amax > 0, np.frexp(amax)[1] - 1 + 127 - 7, 1), 1, 254)
    codes = (b * np.exp2(127.0 - byte)[:, None, :]).reshape(n, m).astype(np.float32).astype(ml_dtypes.float8_e4m3fn).view(np.uint8)
    words = codes.reshape(n // 512, 128, 4, m).transpose(0, 1, 3, 2)
    return np.ascontiguousarray(words), np.ascontiguousarray(byte.astype(np.uint8).reshape(n // 512, 16, m))


K, T, S, H, T2, P = 512, 4096, 1024, 1024, 2048, 1024

def setup_inputs():
    n = np.random.standard_normal
    s = mx_kscale(K)[:, None]
    u = mx_kscale(H)[:, None]
    tab_words, tab_scales = pack_weight(n((K, T)) * s, "e4m3")
    w2_words, w2_scales = pack_weight(0.8 * n((K, H)) / s / np.sqrt(K), "e4m3")
    size = np.exp(0.8 * n(H))
    w4_words, w4_scales = pack_weight(0.7 * n((H, H)) * size / u / np.sqrt(H), "e2m1")
    return {
        "tab_words": tab_words, "tab_scales": tab_scales,
        "offs": striped(np.random.permutation(T)[:S]),
        "w1": (1.5 * n((K, H)) / s / np.sqrt(K)).astype(np.float32),
        "w2_words": w2_words, "w2_scales": w2_scales,
        "w3": (0.52 * n((K, H)) / s / np.sqrt(K)).astype(np.float32),
        "wgs": np.repeat(np.random.uniform(0.5, 2.0, (8, S)), 16, axis=0).astype(np.float32),
        "offs2": striped8(np.stack([np.random.permutation(T2)[:S] for _ in range(8)])),
        "offs3": striped(np.random.permutation(T2)[:P]),
        "gain": (np.exp(0.3 * n(H)) * u[:, 0]).astype(np.float32),
        "jam": (0.7 * n((H, P)) * u).astype(np.float32),
        "w4_words": w4_words, "w4_scales": w4_scales,
    }

def reference(tab_words, tab_scales, offs, w1, w2_words, w2_scales, w3, wgs, offs2, offs3, gain, jam, w4_words, w4_scales):
    v = unpack_weight(tab_words, tab_scales, "e4m3")[:, unstriped(offs)]
    w2 = unpack_weight(w2_words, w2_scales, "e4m3")
    w4 = unpack_weight(w4_words, w4_scales, "e2m1")
    y1 = mxq(f64(w1), 0, "e4m3").T @ v
    y2 = w2.T @ v
    y3 = mxq(f64(w3), 0, "e4m3").T @ v
    h = (np.tanh(y1) + y2) * np.cos(y3)
    page = put_heads(h, f64(wgs), unstriped8(offs2), T2)
    x = page[:, unstriped(offs3)]
    z = f64(gain)[:, None] * x + f64(jam)
    zq = mxq(z, 0, "e4m3")
    y = (w4.T @ zq) + x
    words, scales = planes(y)
    return y, words, scales

@@ -1,0 +1,315 @@
+import math
+from contextlib import ExitStack
+
+import concourse.mybir as mybir
+
+K, T, S, H, T2, M = 512, 4096, 1024, 1024, 2048, 1024
+FLOPS = 2 * (3 * K * H * S + H * H * M)
+
+F32 = mybir.dt.float32
+BF16 = mybir.dt.bfloat16
+I32 = mybir.dt.int32
+U32 = mybir.dt.uint32
+U16 = mybir.dt.uint16
+U8 = mybir.dt.uint8
+FP8X4 = mybir.dt.float8_e4m3fn_x4
+FP4X4 = mybir.dt.float4_e2m1fn_x4
+ACT = mybir.ActivationFunctionType
+ALU = mybir.AluOpType
+
+P = 128
+PACK = 4
+GROUP = P * PACK
+GROUPS = H // GROUP
+HALF = 512
+CH = 256
+NCH = M // CH
+
+
+def tile_list_null_slot_features_kernel(
+    tc, tab_words, tab_scales, offs, w1, w2_words, w2_scales, w3, wgs, offs2, offs3, gain, jam,
+    w4_words, w4_scales, out_0, out_1, out_2,
+):
+    nc = tc.nc
+    with ExitStack() as ctx:
+        keep = ctx.enter_context(tc.tile_pool(name="keep", bufs=1))
+        ring = ctx.enter_context(tc.tile_pool(name="ring", bufs=2))
+        psum = ctx.enter_context(tc.psum_pool(name="psum", bufs=8))
+
+        def held(shape, dtype, name):
+            return keep.tile(shape, dtype, name=name, align_bytes=64)
+
+        list1 = keep.tile([P, S // 16], U16, name="list1")
+        list2 = keep.tile([P, S // 16], U16, name="list2")
+        list3 = keep.tile([P, M // 16], U16, name="list3")
+        tab_w = held([P, T], I32, "tab_w")
+        tab_s = held([P, T], U8, "tab_s")
+        v_w = held([P, S], U32, "v_w")
+        v_s = held([P, S], U8, "v_s")
+        w2_s_raw = held([P, H], U8, "w2_s_raw")
+        w4_s_raw = held([P, GROUPS, H], U8, "w4_s_raw")
+        w2_raw = [held([P, GROUP], I32, "w2_raw%d" % b) for b in range(GROUPS)]
+        w4_raw = held([P, GROUPS, 2 * H], U8, "w4_raw")
+        w1_c = held([P, H], I32, "w1_c")
+        w1_s = held([P, H], U8, "w1_s")
+        w3_c = held([P, H], I32, "w3_c")
+        w3_s = held([P, H], U8, "w3_s")
+        wgs_sb = [held([P, HALF], F32, "wgs%d" % hh) for hh in range(2)]
+        gain_sb = held([P, GROUPS, PACK], F32, "gain_sb")
+        pages = [held([P, T2], F32, "page%d" % i) for i in range(2)]
+        x = [held([P, PACK, M], F32, "x%d" % b) for b in range(GROUPS)]
+        z_c = [held([P, M], I32, "z_c%d" % b) for b in range(GROUPS)]
+        z_s = [held([P, M], U8, "z_s%d" % b) for b in range(GROUPS)]
+        y_s = held([P, GROUPS, M], U8, "y_s")
+        zero_in = held([P, 1], F32, "zero_in")
+        zero = held([P, 1], F32, "zero")
+
+        def bank():
+            return psum.tile([P, 512], F32, name="bank")
+
+        nc.vector.memset(tab_s[:].bitcast(I32), 0)
+        nc.vector.memset(zero_in[:], 0.0)
+        nc.gpsimd.memset(w2_s_raw[:].bitcast(I32), 0)
+        nc.gpsimd.memset(w4_s_raw[:].rearrange("p a c -> p (a c)").bitcast(I32), 0)
+        nc.vector.memset(pages[0][:], 0.0)
+        nc.scalar.activation(zero[:], zero_in[:], ACT.Silu)
+
+        def load_raw(w, b):
+            raw = ring.tile([P, PACK, GROUP], F32, name="w_raw")
+            nc.sync.dma_start(
+                out=raw[:],
+                in_=w[:, b * GROUP:(b + 1) * GROUP].rearrange("(p j) c -> p j c", j=PACK),
+            )
+            return raw
+
+        def load_w2(b):
+            nc.sync.dma_start(
+                out=w2_raw[b][:],
+                in_=w2_words[0, :, b * GROUP:(b + 1) * GROUP, :].rearrange("p c i -> p (c i)").bitcast(I32),
+            )
+
+        tab_s_in = ring.tile([P, T // 4], I32, name="tab_s_in", tag="h", align_bytes=64)
+        nc.sync.dma_start(list1[:], offs)
+        for q in range(4):
+            nc.sync.dma_start(
+                out=tab_s_in[32 * q:32 * q + 4, :], in_=tab_scales[0, 4 * q:4 * q + 4, :].bitcast(I32)
+            )
+        nc.sync.dma_start(out=tab_w[:], in_=tab_words[0].rearrange("p t i -> p (t i)").bitcast(I32))
+        w3_raw0 = load_raw(w3, 0)
+        w1_raw0 = load_raw(w1, 0)
+        load_w2(0)
+        for q in range(4):
+            nc.sync.dma_start(
+                out=w2_s_raw[32 * q:32 * q + 4, :].bitcast(I32), in_=w2_scales[0, 4 * q:4 * q + 4, :].bitcast(I32)
+            )
+        nc.gpsimd.memset(pages[1][:], 0.0)
+        nc.sync.dma_start(out=wgs_sb[0][:], in_=wgs[:, 0:HALF])
+        nc.sync.dma_start(list2[:], offs2)
+        nc.sync.dma_start(out=wgs_sb[1][:], in_=wgs[:, HALF:S])
+        nc.sync.dma_start(list3[:], offs3)
+        nc.sync.dma_start(out=gain_sb[:], in_=gain.rearrange("(b p i) -> p b i", p=P, i=PACK))
+        for q in range(4):
+            nc.vector.tensor_copy(tab_s[32 * q:32 * q + 4, :].bitcast(I32), tab_s_in[32 * q:32 * q + 4, :])
+
+        nc.vector.tensor_copy(v_s[:], tab_s[:].indirect(list1[:]))
+        for hh in range(2):
+            nc.vector.tensor_copy(
+                v_w[:, hh * HALF:(hh + 1) * HALF],
+                tab_w[:].bitcast(U32).indirect(list1[:, hh * (HALF // 16):(hh + 1) * (HALF // 16)]),
+            )
+
+        def quantise_weight(raw, codes, scales, b, copy, cuts, grouped):
+            copy(
+                grouped.rearrange("p (t m j) -> p m j t", t=PACK, j=PACK),
+                raw[:].rearrange("p j (m t) -> p m j t", t=PACK),
+            )
+            for lo, hi in zip(cuts[:-1], cuts[1:]):
+                cols = slice(b * GROUP + lo, b * GROUP + hi)
+                nc.vector.quantize_mx(
+                    out=codes[:, cols].bitcast(FP8X4), scales=scales[:, cols], in_=grouped[:, PACK * lo:PACK * hi]
+                )
+
+        w2_c, w2_s = {}, {}
+
+        def deal_w2(b, eng, tags):
+            cols = slice(b * GROUP, (b + 1) * GROUP)
+            w2_c[b] = keep.tile([P, GROUP], I32, name="w2_c", tag=tags[0], align_bytes=64)
+            w2_s[b] = keep.tile([P, GROUP], U8, name="w2_s", tag=tags[1], align_bytes=64)
+            eng.tensor_copy(
+                w2_c[b][:].rearrange("p (t q) -> p q t", t=PACK), w2_raw[b][:].rearrange("p (q t) -> p q t", t=PACK)
+            )
+            eng.tensor_copy(
+                w2_s[b][:].rearrange("p (t q) -> p q t", t=PACK),
+                w2_s_raw[:, cols].rearrange("p (q t) -> p q t", t=PACK),
+            )
+
+        def deal_w4(a, g, eng, w4_c, w4_s):
+            by = slice(2 * g * GROUP, 2 * (g + 1) * GROUP)
+            cols = slice(g * GROUP, (g + 1) * GROUP)
+            eng.tensor_copy(
+                w4_c[:, a, by].bitcast(U16).rearrange("p (t q) -> p q t", t=PACK),
+                w4_raw[:, a, by].bitcast(U16).rearrange("p (q t) -> p q t", t=PACK),
+            )
+            eng.tensor_copy(
+                w4_s[:, a, cols].rearrange("p (t q) -> p q t", t=PACK),
+                w4_s_raw[:, a, cols].rearrange("p (q t) -> p q t", t=PACK),
+            )
+
+        w3_bf = ring.tile([P, GROUP * PACK], BF16, name="w3_bf", tag="h", align_bytes=64)
+        quantise_weight(w3_raw0, w3_c, w3_s, 0, nc.vector.tensor_copy, [0, GROUP], w3_bf[:])
+        w1_bf = ring.tile([P, GROUP * PACK], BF16, name="w1_bf", tag="h", align_bytes=64)
+        quantise_weight(w1_raw0, w1_c, w1_s, 0, nc.vector.tensor_copy, [0, P, GROUP], w1_bf[:])
+        deal_w2(0, nc.vector, ["w2_c0", "w2_s0"])
+
+        def product(codes, scales, s, hh):
+            acc = bank()
+            wc = slice(s * P, (s + 1) * P)
+            vc = slice(hh * HALF, (hh + 1) * HALF)
+            nc.tensor.matmul_mx(
+                out=acc[:], lhsT=codes[:, wc].bitcast(FP8X4), lhsT_scale=scales[:, wc],
+                rhs=v_w[:, vc].bitcast(FP8X4), rhs_scale=v_s[:, vc], start=True, stop=True,
+            )
+            return acc
+
+        def features(s, first):
+            page = pages[s % 2]
+            if first:
+                th = keep.tile([P, S], F32, name="th", tag="late_w2_c", align_bytes=64)
+                cs = keep.tile([P, S], F32, name="cs", tag="late_w2_s", align_bytes=64)
+            else:
+                th = ring.tile([P, S], F32, name="th", bufs=3, align_bytes=64)
+                cs = ring.tile([P, S], F32, name="cs")
+            if s == 1:
+                y2 = keep.tile([P, S], F32, name="y2", tag="late_w4_c", align_bytes=64)
+                h = keep.tile([P, S], F32, name="h", tag="late_w4_s", align_bytes=64)
+            elif not first:
+                y2 = ring.tile([P, S], F32, name="y2", bufs=3)
+                h = ring.tile([P, S], F32, name="h", align_bytes=64)
+            for hh in range(2):
+                vc = slice(hh * HALF, (hh + 1) * HALF)
+                nc.scalar.activation(cs[:, vc], product(w3_c, w3_s, s, hh)[:], ACT.Abs, bias=zero[:])
+                nc.scalar.activation(cs[:, vc], cs[:, vc], ACT.Sin, scale=-1.0, bias=math.pi / 2)
+                nc.scalar.activation(th[:, vc], product(w1_c, w1_s, s, hh)[:], ACT.Tanh, bias=zero[:])
+                acc2 = product(w2_c[s // PACK], w2_s[s // PACK], s % PACK, hh)
+                if first:
+                    nc.vector.tensor_tensor(cs[:, vc], cs[:, vc], wgs_sb[hh][:], ALU.mult)
+                    nc.vector.tensor_tensor(th[:, vc], acc2[:], th[:, vc], ALU.add)
+                    nc.vector.tensor_tensor(
+                        page[:].indirect(list2[:, hh * (HALF // 16):(hh + 1) * (HALF // 16)]),
+                        th[:, vc], cs[:, vc], ALU.mult,
+                    )
+                else:
+                    nc.scalar.copy(y2[:, vc], acc2[:])
+                    nc.gpsimd.tensor_tensor(cs[:, vc], cs[:, vc], wgs_sb[hh][:], ALU.mult)
+            if not first:
+                nc.gpsimd.tensor_tensor(th[:], th[:], y2[:], ALU.add)
+                nc.gpsimd.tensor_tensor(h[:], th[:], cs[:], ALU.mult)
+                nc.vector.tensor_copy(page[:].indirect(list2[:]), h[:])
+                return th, cs, y2
+            return th, cs, None
+
+        z_planes = {}
+
+        def read_slots(s, widths):
+            b, t = divmod(s, PACK)
+            for lo in range(0, M, widths):
+                nc.vector.tensor_copy(
+                    x[b][:, t, lo:lo + widths], pages[s % 2][:].indirect(list3[:, lo // 16:(lo + widths) // 16])
+                )
+
+        def join_jam(s, widths, gx):
+            b, t = divmod(s, PACK)
+            if t == 0:
+                z_planes[b] = keep.tile([P, PACK, M], BF16, name="z_planes", align_bytes=64)
+            jam_sb = ring.tile([P, M], F32, name="jam_sb", bufs=4)
+            nc.sync.dma_start(
+                out=jam_sb[:], in_=jam[b * GROUP:(b + 1) * GROUP, :].rearrange("(p t) m -> p t m", t=PACK)[:, t, :]
+            )
+            for lo in range(0, M, widths):
+                mc = slice(lo, lo + widths)
+                nc.scalar.activation(gx[:, mc], x[b][:, t, mc], ACT.Copy, scale=gain_sb[:, b, t:t + 1])
+                nc.gpsimd.tensor_tensor(z_planes[b][:, t, mc], gx[:, mc], jam_sb[:, mc], ALU.add)
+
+        def weave(dst, src):
+            nc.scalar.copy(
+                dst.rearrange("p (c i t) -> p c t i", i=4, t=PACK), src.rearrange("p t (c i) -> p c t i", i=4)
+            )
+
+        def quantise_z(b, c):
+            mc = slice(c * CH, (c + 1) * CH)
+            z_bf = ring.tile([P, CH * PACK], BF16, name="z_bf", align_bytes=64)
+            weave(z_bf[:], z_planes[b][:, :, mc])
+            nc.vector.quantize_mx(out=z_c[b][:, mc].bitcast(FP8X4), scales=z_s[b][:, mc], in_=z_bf[:])
+
+        for s in range(GROUPS * PACK):
+            th, cs, y2 = features(s, s == 0)
+            read_slots(s, CH if s == GROUPS * PACK - 1 else M)
+            if s >= 2:
+                join_jam(s - 2, M, y2)
+            if s == 0:
+                w3_raw1 = load_raw(w3, 1)
+                w1_raw1 = load_raw(w1, 1)
+                load_w2(1)
+                nc.sync.dma_start(
+                    out=w4_raw[:].bitcast(I32), in_=w4_words.rearrange("a p c -> p a c").bitcast(I32)
+                )
+                for q in range(4):
+                    nc.sync.dma_start(
+                        out=w4_s_raw[32 * q:32 * q + 4, :, :].bitcast(I32),
+                        in_=w4_scales[:, 4 * q:4 * q + 4, :].rearrange("a r c -> r a c").bitcast(I32),
+                    )
+            if s == 1:
+                quantise_weight(w3_raw1, w3_c, w3_s, 1, nc.scalar.copy, [0, GROUP], th[:].bitcast(BF16))
+                deal_w2(1, nc.vector, ["late_w2_c", "late_w2_s"])
+            if s == 2:
+                quantise_weight(w1_raw1, w1_c, w1_s, 1, nc.scalar.copy, [0, GROUP], th[:].bitcast(BF16))
+                w4_c = keep.tile([P, GROUPS, 2 * H], U8, name="w4_c", tag="late_w4_c", align_bytes=64)
+                w4_s = keep.tile([P, GROUPS, H], U8, name="w4_s", tag="late_w4_s", align_bytes=64)
+            if s == 5:
+                for c in range(NCH):
+                    quantise_z(0, c)
+            if s >= 4:
+                deal_w4((s - 4) // 2, (s - 4) % 2, nc.vector, w4_c, w4_s)
+
+        join_jam(6, M, cs)
+        join_jam(7, CH, th)
+        for c in range(NCH):
+            quantise_z(1, c)
+        for c in range(NCH):
+            mc = slice(c * CH, (c + 1) * CH)
+            for g in range(GROUPS):
+                y = ring.tile([P, PACK, CH], F32, name="y", tag="jam_sb", bufs=4)
+                for pair in range(2):
+                    acc = bank()
+                    for e in range(2):
+                        t = 2 * pair + e
+                        col = g * GROUP + t * P
+                        for a in range(GROUPS):
+                            nc.tensor.matmul_mx(
+                                out=acc[:, e * CH:(e + 1) * CH],
+                                lhsT=w4_c[:, a, 2 * col:2 * (col + P)].bitcast(FP4X4),
+                                lhsT_scale=w4_s[:, a, col:col + P],
+                                rhs=z_c[a][:, mc].bitcast(FP8X4), rhs_scale=z_s[a][:, mc],
+                                start=(a == 0), stop=(a == GROUPS - 1),
+                            )
+                    nc.vector.tensor_tensor(
+                        y[:, 2 * pair:2 * pair + 2, :],
+                        acc[:].rearrange("p (e m) -> p e m", e=2),
+                        x[g][:, 2 * pair:2 * pair + 2, mc],
+                        ALU.add,
+                    )
+                nc.sync.dma_start(
+                    out=out_0[g * GROUP:(g + 1) * GROUP, mc].rearrange("(p t) m -> p t m", t=PACK), in_=y[:]
+                )
+                y_bf = ring.tile([P, CH * PACK], BF16, name="y_bf", bufs=3, align_bytes=64)
+                weave(y_bf[:], y[:])
+                y_c = ring.tile([P, CH], I32, name="y_c", bufs=3, align_bytes=64)
+                nc.vector.quantize_mx(out=y_c[:].bitcast(FP8X4), scales=y_s[:, g, mc], in_=y_bf[:])
+                nc.sync.dma_start(
+                    out=out_1[g, :, mc, :].rearrange("p m t -> p (m t)").bitcast(I32), in_=y_c[:]
+                )
+        for q in range(4):
+            nc.sync.dma_start(
+                out=out_2[:, 4 * q:4 * q + 4, :].rearrange("g r m -> r g m").bitcast(I32),
+                in_=y_s[32 * q:32 * q + 4, :, :].bitcast(I32),
+            )

@@ -21,9 +21,18 @@ P = 128
 PACK = 4
 GROUP = P * PACK
 GROUPS = H // GROUP
+SLICES = GROUPS * PACK
 HALF = 512
 CH = 256
 NCH = M // CH
+V_ADD = ()
+G_WEAVE = ()
+V_WEAVE = (7,)
+SPLIT = 80
+SPLITS = (0,96)
+WHOLE = (True,False)
+HOLD = "y2"
+Z0_LATE = False
 
 
 def tile_list_null_slot_features_kernel(
@@ -36,8 +45,8 @@ def tile_list_null_slot_features_kernel(
         ring = ctx.enter_context(tc.tile_pool(name="ring", bufs=2))
         psum = ctx.enter_context(tc.psum_pool(name="psum", bufs=8))
 
-        def held(shape, dtype, name):
-            return keep.tile(shape, dtype, name=name, align_bytes=64)
+        def held(shape, dtype, name, tag=None):
+            return keep.tile(shape, dtype, name=name, tag=tag or name, align_bytes=64)
 
         list1 = keep.tile([P, S // 16], U16, name="list1")
         list2 = keep.tile([P, S // 16], U16, name="list2")
@@ -48,30 +57,36 @@ def tile_list_null_slot_features_kernel(
         v_s = held([P, S], U8, "v_s")
         w2_s_raw = held([P, H], U8, "w2_s_raw")
         w4_s_raw = held([P, GROUPS, H], U8, "w4_s_raw")
-        w2_raw = [held([P, GROUP], I32, "w2_raw%d" % b) for b in range(GROUPS)]
+        w2_raw = held([P, H], I32, "w2_raw")
         w4_raw = held([P, GROUPS, 2 * H], U8, "w4_raw")
-        w1_c = held([P, H], I32, "w1_c")
-        w1_s = held([P, H], U8, "w1_s")
-        w3_c = held([P, H], I32, "w3_c")
-        w3_s = held([P, H], U8, "w3_s")
-        wgs_sb = [held([P, HALF], F32, "wgs%d" % hh) for hh in range(2)]
+        w31_c = [held([P, 2 * GROUP], I32, "w31_c%d" % b) for b in range(GROUPS)]
+        w31_s = [held([P, 2 * GROUP], U8, "w31_s%d" % b) for b in range(GROUPS)]
+        w2_c = held([P, H], I32, "w2_c")
+        w2_s = held([P, H], U8, "w2_s")
+        wgs_sb = held([P, S], F32, "wgs_sb")
         gain_sb = held([P, GROUPS, PACK], F32, "gain_sb")
         pages = [held([P, T2], F32, "page%d" % i) for i in range(2)]
         x = [held([P, PACK, M], F32, "x%d" % b) for b in range(GROUPS)]
         z_c = [held([P, M], I32, "z_c%d" % b) for b in range(GROUPS)]
         z_s = [held([P, M], U8, "z_s%d" % b) for b in range(GROUPS)]
         y_s = held([P, GROUPS, M], U8, "y_s")
+        cos_w = held([P, S], F32, "cos_w")
+        amp = held([P, S], F32, "amp")
         zero_in = held([P, 1], F32, "zero_in")
         zero = held([P, 1], F32, "zero")
 
         def bank():
             return psum.tile([P, 512], F32, name="bank")
 
-        nc.vector.memset(tab_s[:].bitcast(I32), 0)
+        def entries(lst, lo, hi):
+            return lst[:, lo // 16:hi // 16]
+
         nc.vector.memset(zero_in[:], 0.0)
-        nc.gpsimd.memset(w2_s_raw[:].bitcast(I32), 0)
-        nc.gpsimd.memset(w4_s_raw[:].rearrange("p a c -> p (a c)").bitcast(I32), 0)
+        nc.vector.memset(w2_s_raw[:].bitcast(I32), 0)
+        nc.vector.memset(tab_s[:].bitcast(I32), 0)
+        nc.vector.memset(w4_s_raw[:].rearrange("p a c -> p (a c)").bitcast(I32), 0)
         nc.vector.memset(pages[0][:], 0.0)
+        nc.vector.memset(pages[1][:], 0.0)
         nc.scalar.activation(zero[:], zero_in[:], ACT.Silu)
 
         def load_raw(w, b):
@@ -82,174 +97,161 @@ def tile_list_null_slot_features_kernel(
             )
             return raw
 
-        def load_w2(b):
-            nc.sync.dma_start(
-                out=w2_raw[b][:],
-                in_=w2_words[0, :, b * GROUP:(b + 1) * GROUP, :].rearrange("p c i -> p (c i)").bitcast(I32),
-            )
-
         tab_s_in = ring.tile([P, T // 4], I32, name="tab_s_in", tag="h", align_bytes=64)
         nc.sync.dma_start(list1[:], offs)
         for q in range(4):
             nc.sync.dma_start(
                 out=tab_s_in[32 * q:32 * q + 4, :], in_=tab_scales[0, 4 * q:4 * q + 4, :].bitcast(I32)
             )
-        nc.sync.dma_start(out=tab_w[:], in_=tab_words[0].rearrange("p t i -> p (t i)").bitcast(I32))
         w3_raw0 = load_raw(w3, 0)
+        nc.sync.dma_start(out=tab_w[:], in_=tab_words[0].rearrange("p t i -> p (t i)").bitcast(I32))
         w1_raw0 = load_raw(w1, 0)
-        load_w2(0)
         for q in range(4):
             nc.sync.dma_start(
                 out=w2_s_raw[32 * q:32 * q + 4, :].bitcast(I32), in_=w2_scales[0, 4 * q:4 * q + 4, :].bitcast(I32)
             )
-        nc.gpsimd.memset(pages[1][:], 0.0)
-        nc.sync.dma_start(out=wgs_sb[0][:], in_=wgs[:, 0:HALF])
+        nc.sync.dma_start(out=w2_raw[:], in_=w2_words[0].rearrange("p c i -> p (c i)").bitcast(I32))
+        nc.sync.dma_start(out=wgs_sb[:, 0:HALF], in_=wgs[:, 0:HALF])
         nc.sync.dma_start(list2[:], offs2)
-        nc.sync.dma_start(out=wgs_sb[1][:], in_=wgs[:, HALF:S])
+        nc.sync.dma_start(out=wgs_sb[:, HALF:S], in_=wgs[:, HALF:S])
         nc.sync.dma_start(list3[:], offs3)
         nc.sync.dma_start(out=gain_sb[:], in_=gain.rearrange("(b p i) -> p b i", p=P, i=PACK))
         for q in range(4):
             nc.vector.tensor_copy(tab_s[32 * q:32 * q + 4, :].bitcast(I32), tab_s_in[32 * q:32 * q + 4, :])
 
         nc.vector.tensor_copy(v_s[:], tab_s[:].indirect(list1[:]))
-        for hh in range(2):
+        for lo in range(0, S, HALF):
             nc.vector.tensor_copy(
-                v_w[:, hh * HALF:(hh + 1) * HALF],
-                tab_w[:].bitcast(U32).indirect(list1[:, hh * (HALF // 16):(hh + 1) * (HALF // 16)]),
+                v_w[:, lo:lo + HALF], tab_w[:].bitcast(U32).indirect(entries(list1, lo, lo + HALF))
             )
 
-        def quantise_weight(raw, codes, scales, b, copy, cuts, grouped):
+        def round_weight(raw, grouped, copy, lo, hi):
             copy(
-                grouped.rearrange("p (t m j) -> p m j t", t=PACK, j=PACK),
-                raw[:].rearrange("p j (m t) -> p m j t", t=PACK),
-            )
-            for lo, hi in zip(cuts[:-1], cuts[1:]):
-                cols = slice(b * GROUP + lo, b * GROUP + hi)
-                nc.vector.quantize_mx(
-                    out=codes[:, cols].bitcast(FP8X4), scales=scales[:, cols], in_=grouped[:, PACK * lo:PACK * hi]
-                )
-
-        w2_c, w2_s = {}, {}
-
-        def deal_w2(b, eng, tags):
-            cols = slice(b * GROUP, (b + 1) * GROUP)
-            w2_c[b] = keep.tile([P, GROUP], I32, name="w2_c", tag=tags[0], align_bytes=64)
-            w2_s[b] = keep.tile([P, GROUP], U8, name="w2_s", tag=tags[1], align_bytes=64)
-            eng.tensor_copy(
-                w2_c[b][:].rearrange("p (t q) -> p q t", t=PACK), w2_raw[b][:].rearrange("p (q t) -> p q t", t=PACK)
-            )
-            eng.tensor_copy(
-                w2_s[b][:].rearrange("p (t q) -> p q t", t=PACK),
-                w2_s_raw[:, cols].rearrange("p (q t) -> p q t", t=PACK),
+                grouped.rearrange("p (t m j) -> p m j t", t=PACK, j=PACK)[:, lo:hi],
+                raw[:].rearrange("p j (m t) -> p m j t", t=PACK)[:, lo:hi],
             )
 
-        def deal_w4(a, g, eng, w4_c, w4_s):
-            by = slice(2 * g * GROUP, 2 * (g + 1) * GROUP)
-            cols = slice(g * GROUP, (g + 1) * GROUP)
-            eng.tensor_copy(
-                w4_c[:, a, by].bitcast(U16).rearrange("p (t q) -> p q t", t=PACK),
-                w4_raw[:, a, by].bitcast(U16).rearrange("p (q t) -> p q t", t=PACK),
-            )
-            eng.tensor_copy(
-                w4_s[:, a, cols].rearrange("p (t q) -> p q t", t=PACK),
-                w4_s_raw[:, a, cols].rearrange("p (q t) -> p q t", t=PACK),
+        def quantise(codes, scales, grouped, lo, hi):
+            nc.vector.quantize_mx(
+                out=codes[:, lo:hi].bitcast(FP8X4), scales=scales[:, lo:hi], in_=grouped[:, PACK * lo:PACK * hi]
             )
 
-        w3_bf = ring.tile([P, GROUP * PACK], BF16, name="w3_bf", tag="h", align_bytes=64)
-        quantise_weight(w3_raw0, w3_c, w3_s, 0, nc.vector.tensor_copy, [0, GROUP], w3_bf[:])
-        w1_bf = ring.tile([P, GROUP * PACK], BF16, name="w1_bf", tag="h", align_bytes=64)
-        quantise_weight(w1_raw0, w1_c, w1_s, 0, nc.vector.tensor_copy, [0, P, GROUP], w1_bf[:])
-        deal_w2(0, nc.vector, ["w2_c0", "w2_s0"])
+        w_bf = x[1][:].rearrange("p t m -> p (t m)").bitcast(BF16)
+        w_bf0, w_bf1 = w_bf[:, 0:2 * GROUP * PACK], w_bf[:, 2 * GROUP * PACK:4 * GROUP * PACK]
+        for i, raw in enumerate((w3_raw0, w1_raw0)):
+            part = w_bf0[:, i * GROUP * PACK:(i + 1) * GROUP * PACK]
+            if SPLITS[i] > 0:
+                round_weight(raw, part, nc.vector.tensor_copy, 0, SPLITS[i])
+            round_weight(raw, part, nc.scalar.copy, SPLITS[i], P)
+            quantise(w31_c[0], w31_s[0], w_bf0, i * GROUP, i * GROUP + (GROUP if WHOLE[i] else P))
+        nc.vector.tensor_copy(
+            w2_s[:].rearrange("p (g t q) -> p g q t", t=PACK, q=P),
+            w2_s_raw[:].rearrange("p (g q t) -> p g q t", t=PACK, q=P),
+        )
+        nc.vector.tensor_copy(
+            w2_c[:].rearrange("p (g t q) -> p g q t", t=PACK, q=P),
+            w2_raw[:].rearrange("p (g q t) -> p g q t", t=PACK, q=P),
+        )
+        for i in range(2):
+            if not WHOLE[i]:
+                quantise(w31_c[0], w31_s[0], w_bf0, i * GROUP + P, (i + 1) * GROUP)
 
-        def product(codes, scales, s, hh):
+        def product(codes, scales, col, lo):
             acc = bank()
-            wc = slice(s * P, (s + 1) * P)
-            vc = slice(hh * HALF, (hh + 1) * HALF)
             nc.tensor.matmul_mx(
-                out=acc[:], lhsT=codes[:, wc].bitcast(FP8X4), lhsT_scale=scales[:, wc],
-                rhs=v_w[:, vc].bitcast(FP8X4), rhs_scale=v_s[:, vc], start=True, stop=True,
+                out=acc[:], lhsT=codes[:, col:col + P].bitcast(FP8X4), lhsT_scale=scales[:, col:col + P],
+                rhs=v_w[:, lo:lo + HALF].bitcast(FP8X4), rhs_scale=v_s[:, lo:lo + HALF], start=True, stop=True,
             )
             return acc
 
-        def features(s, first):
+        def features(s):
+            b, t = divmod(s, PACK)
             page = pages[s % 2]
-            if first:
-                th = keep.tile([P, S], F32, name="th", tag="late_w2_c", align_bytes=64)
-                cs = keep.tile([P, S], F32, name="cs", tag="late_w2_s", align_bytes=64)
-            else:
-                th = ring.tile([P, S], F32, name="th", bufs=3, align_bytes=64)
-                cs = ring.tile([P, S], F32, name="cs")
-            if s == 1:
-                y2 = keep.tile([P, S], F32, name="y2", tag="late_w4_c", align_bytes=64)
-                h = keep.tile([P, S], F32, name="h", tag="late_w4_s", align_bytes=64)
-            elif not first:
+            th = ring.tile([P, S], F32, name="th", bufs=2)
+            cs = ring.tile([P, S], F32, name="cs", bufs=2)
+            y2 = None
+            if s > 0:
                 y2 = ring.tile([P, S], F32, name="y2", bufs=3)
+            if s == SLICES - 1:
+                h = held([P, S], F32, "h", "late_w4")
+            else:
                 h = ring.tile([P, S], F32, name="h", align_bytes=64)
-            for hh in range(2):
-                vc = slice(hh * HALF, (hh + 1) * HALF)
-                nc.scalar.activation(cs[:, vc], product(w3_c, w3_s, s, hh)[:], ACT.Abs, bias=zero[:])
-                nc.scalar.activation(cs[:, vc], cs[:, vc], ACT.Sin, scale=-1.0, bias=math.pi / 2)
-                nc.scalar.activation(th[:, vc], product(w1_c, w1_s, s, hh)[:], ACT.Tanh, bias=zero[:])
-                acc2 = product(w2_c[s // PACK], w2_s[s // PACK], s % PACK, hh)
-                if first:
-                    nc.vector.tensor_tensor(cs[:, vc], cs[:, vc], wgs_sb[hh][:], ALU.mult)
-                    nc.vector.tensor_tensor(th[:, vc], acc2[:], th[:, vc], ALU.add)
-                    nc.vector.tensor_tensor(
-                        page[:].indirect(list2[:, hh * (HALF // 16):(hh + 1) * (HALF // 16)]),
-                        th[:, vc], cs[:, vc], ALU.mult,
-                    )
-                else:
-                    nc.scalar.copy(y2[:, vc], acc2[:])
-                    nc.gpsimd.tensor_tensor(cs[:, vc], cs[:, vc], wgs_sb[hh][:], ALU.mult)
-            if not first:
-                nc.gpsimd.tensor_tensor(th[:], th[:], y2[:], ALU.add)
-                nc.gpsimd.tensor_tensor(h[:], th[:], cs[:], ALU.mult)
+            halves = [slice(lo, lo + HALF) for lo in range(0, S, HALF)]
+            if s == 0:
+                for vc in halves:
+                    phase = product(w31_c[b], w31_s[b], t * P, vc.start)
+                    nc.scalar.activation(cs[:, vc], phase[:], ACT.Abs, bias=zero[:])
+                    nc.scalar.activation(cs[:, vc], cs[:, vc], ACT.Sin, scale=-1.0, bias=math.pi / 2)
+                    gate = product(w31_c[b], w31_s[b], GROUP + t * P, vc.start)
+                    nc.scalar.activation(th[:, vc], gate[:], ACT.Tanh, bias=zero[:])
+                nc.vector.tensor_tensor(cos_w[:], cs[:], wgs_sb[:], ALU.mult)
+                for vc in halves:
+                    nc.vector.tensor_tensor(amp[:, vc], product(w2_c, w2_s, s * P, vc.start)[:], th[:, vc], ALU.add)
+                for vc, eng in zip(halves, (nc.vector, nc.gpsimd)):
+                    eng.tensor_tensor(h[:, vc], amp[:, vc], cos_w[:, vc], ALU.mult)
+                    nc.vector.tensor_copy(page[:].indirect(entries(list2, vc.start, vc.stop)), h[:, vc])
+            else:
+                for vc in halves:
+                    phase = product(w31_c[b], w31_s[b], t * P, vc.start)
+                    nc.scalar.activation(cs[:, vc], phase[:], ACT.Abs, bias=zero[:])
+                nc.scalar.activation(cs[:], cs[:], ACT.Sin, scale=-1.0, bias=math.pi / 2)
+                for vc in halves:
+                    gate = product(w31_c[b], w31_s[b], GROUP + t * P, vc.start)
+                    nc.scalar.activation(th[:, vc], gate[:], ACT.Tanh, bias=zero[:])
+                    nc.scalar.copy(y2[:, vc], product(w2_c, w2_s, s * P, vc.start)[:])
+            if s > 0:
+                nc.gpsimd.tensor_tensor(cos_w[:], cs[:], wgs_sb[:], ALU.mult)
+                nc.gpsimd.tensor_tensor(amp[:], th[:], y2[:], ALU.add)
+                nc.gpsimd.tensor_tensor(h[:], amp[:], cos_w[:], ALU.mult)
                 nc.vector.tensor_copy(page[:].indirect(list2[:]), h[:])
-                return th, cs, y2
-            return th, cs, None
+            return th, cs, y2
 
         z_planes = {}
 
-        def read_slots(s, widths):
+        def read_slots(s, width):
             b, t = divmod(s, PACK)
-            for lo in range(0, M, widths):
+            for lo in range(0, M, width):
                 nc.vector.tensor_copy(
-                    x[b][:, t, lo:lo + widths], pages[s % 2][:].indirect(list3[:, lo // 16:(lo + widths) // 16])
+                    x[b][:, t, lo:lo + width], pages[s % 2][:].indirect(entries(list3, lo, lo + width))
                 )
 
-        def join_jam(s, widths, gx):
+        def join_jam(s, width, gx):
             b, t = divmod(s, PACK)
             if t == 0:
-                z_planes[b] = keep.tile([P, PACK, M], BF16, name="z_planes", align_bytes=64)
+                z_planes[b] = held([P, PACK, M], BF16, "z_planes")
             jam_sb = ring.tile([P, M], F32, name="jam_sb", bufs=4)
             nc.sync.dma_start(
                 out=jam_sb[:], in_=jam[b * GROUP:(b + 1) * GROUP, :].rearrange("(p t) m -> p t m", t=PACK)[:, t, :]
             )
-            for lo in range(0, M, widths):
-                mc = slice(lo, lo + widths)
-                nc.scalar.activation(gx[:, mc], x[b][:, t, mc], ACT.Copy, scale=gain_sb[:, b, t:t + 1])
-                nc.gpsimd.tensor_tensor(z_planes[b][:, t, mc], gx[:, mc], jam_sb[:, mc], ALU.add)
+            for lo in range(0, M, width):
+                mc = slice(lo, lo + width)
+                if gx is None:
+                    nc.vector.scalar_tensor_tensor(
+                        out=z_planes[b][:, t, mc], in0=x[b][:, t, mc], scalar=gain_sb[:, b, t:t + 1],
+                        in1=jam_sb[:, mc], op0=ALU.mult, op1=ALU.add,
+                    )
+                else:
+                    nc.scalar.activation(gx[:, mc], x[b][:, t, mc], ACT.Copy, scale=gain_sb[:, b, t:t + 1])
+                    nc.gpsimd.tensor_tensor(z_planes[b][:, t, mc], gx[:, mc], jam_sb[:, mc], ALU.add)
 
-        def weave(dst, src):
-            nc.scalar.copy(
-                dst.rearrange("p (c i t) -> p c t i", i=4, t=PACK), src.rearrange("p t (c i) -> p c t i", i=4)
-            )
+        def weave(dst, src, eng):
+            dst = dst.rearrange("p (c i t) -> p c t i", i=4, t=PACK)
+            src = src.rearrange("p t (c i) -> p c t i", i=4)
+            if eng == "g":
+                nc.gpsimd.tensor_scalar(dst, src, 1.0, 0.0, ALU.mult, ALU.add)
+            elif eng == "v":
+                nc.vector.tensor_copy(dst, src)
+            else:
+                nc.scalar.copy(dst, src)
 
-        def quantise_z(b, c):
-            mc = slice(c * CH, (c + 1) * CH)
-            z_bf = ring.tile([P, CH * PACK], BF16, name="z_bf", align_bytes=64)
-            weave(z_bf[:], z_planes[b][:, :, mc])
-            nc.vector.quantize_mx(out=z_c[b][:, mc].bitcast(FP8X4), scales=z_s[b][:, mc], in_=z_bf[:])
-
-        for s in range(GROUPS * PACK):
-            th, cs, y2 = features(s, s == 0)
-            read_slots(s, CH if s == GROUPS * PACK - 1 else M)
+        for s in range(SLICES):
+            th, cs, y2 = features(s)
+            read_slots(s, CH if s == SLICES - 1 else M)
             if s >= 2:
-                join_jam(s - 2, M, y2)
+                join_jam(s - 2, M, y2 if (HOLD == "y2" and y2 is not None) else cs)
             if s == 0:
                 w3_raw1 = load_raw(w3, 1)
                 w1_raw1 = load_raw(w1, 1)
-                load_w2(1)
                 nc.sync.dma_start(
                     out=w4_raw[:].bitcast(I32), in_=w4_words.rearrange("a p c -> p a c").bitcast(I32)
                 )
@@ -258,23 +260,37 @@ def tile_list_null_slot_features_kernel(
                         out=w4_s_raw[32 * q:32 * q + 4, :, :].bitcast(I32),
                         in_=w4_scales[:, 4 * q:4 * q + 4, :].rearrange("a r c -> r a c").bitcast(I32),
                     )
-            if s == 1:
-                quantise_weight(w3_raw1, w3_c, w3_s, 1, nc.scalar.copy, [0, GROUP], th[:].bitcast(BF16))
-                deal_w2(1, nc.vector, ["late_w2_c", "late_w2_s"])
             if s == 2:
-                quantise_weight(w1_raw1, w1_c, w1_s, 1, nc.scalar.copy, [0, GROUP], th[:].bitcast(BF16))
-                w4_c = keep.tile([P, GROUPS, 2 * H], U8, name="w4_c", tag="late_w4_c", align_bytes=64)
-                w4_s = keep.tile([P, GROUPS, H], U8, name="w4_s", tag="late_w4_s", align_bytes=64)
+                for i, raw in enumerate((w3_raw1, w1_raw1)):
+                    round_weight(raw, w_bf1[:, i * GROUP * PACK:(i + 1) * GROUP * PACK], nc.scalar.copy, 0, P)
+                quantise(w31_c[1], w31_s[1], w_bf1, 0, 2 * GROUP)
             if s == 5:
-                for c in range(NCH):
-                    quantise_z(0, c)
-            if s >= 4:
-                deal_w4((s - 4) // 2, (s - 4) % 2, nc.vector, w4_c, w4_s)
+                z0_bf = held([P, M * PACK], BF16, "z0_bf", "tab_w")
+                for c in range(4):
+                    weave(z0_bf[:, c * M:(c + 1) * M], z_planes[0][:, :, c * 256:(c + 1) * 256], "s")
+                if not Z0_LATE:
+                    quantise(z_c[0], z_s[0], z0_bf, 0, M)
 
-        join_jam(6, M, cs)
-        join_jam(7, CH, th)
+        join_jam(6, M, amp)
+        join_jam(7, CH, None)
+        w4_cs = held([P, 3 * GROUPS * H], U8, "w4_cs", "late_w4")
+        w4_c = w4_cs[:, 0:2 * GROUPS * H].rearrange("p (a c) -> p a c", a=GROUPS)
+        w4_s = w4_cs[:, 2 * GROUPS * H:3 * GROUPS * H].rearrange("p (a c) -> p a c", a=GROUPS)
+        for g in range(GROUPS):
+            nc.vector.tensor_copy(
+                w4_c[:, :, 2 * g * GROUP:2 * (g + 1) * GROUP].bitcast(U16).rearrange("p a (t q) -> p a q t", t=PACK),
+                w4_raw[:, :, 2 * g * GROUP:2 * (g + 1) * GROUP].bitcast(U16).rearrange("p a (q t) -> p a q t", t=PACK),
+            )
+            nc.vector.tensor_copy(
+                w4_s[:, :, g * GROUP:(g + 1) * GROUP].rearrange("p a (t q) -> p a q t", t=PACK),
+                w4_s_raw[:, :, g * GROUP:(g + 1) * GROUP].rearrange("p a (q t) -> p a q t", t=PACK),
+            )
         for c in range(NCH):
-            quantise_z(1, c)
+            z_bf = ring.tile([P, CH * PACK], BF16, name="z_bf", bufs=4, align_bytes=64)
+            weave(z_bf[:], z_planes[1][:, :, c * CH:(c + 1) * CH], "s")
+            nc.vector.quantize_mx(
+                out=z_c[1][:, c * CH:(c + 1) * CH].bitcast(FP8X4), scales=z_s[1][:, c * CH:(c + 1) * CH], in_=z_bf[:]
+            )
         for c in range(NCH):
             mc = slice(c * CH, (c + 1) * CH)
             for g in range(GROUPS):
@@ -282,8 +298,7 @@ def tile_list_null_slot_features_kernel(
                 for pair in range(2):
                     acc = bank()
                     for e in range(2):
-                        t = 2 * pair + e
-                        col = g * GROUP + t * P
+                        col = g * GROUP + (2 * pair + e) * P
                         for a in range(GROUPS):
                             nc.tensor.matmul_mx(
                                 out=acc[:, e * CH:(e + 1) * CH],
@@ -302,7 +317,8 @@ def tile_list_null_slot_features_kernel(
                     out=out_0[g * GROUP:(g + 1) * GROUP, mc].rearrange("(p t) m -> p t m", t=PACK), in_=y[:]
                 )
                 y_bf = ring.tile([P, CH * PACK], BF16, name="y_bf", bufs=3, align_bytes=64)
-                weave(y_bf[:], y[:])
+                n = GROUPS * c + g
+                weave(y_bf[:], y[:], "g" if n in G_WEAVE else "v" if n in V_WEAVE else "s")
                 y_c = ring.tile([P, CH], I32, name="y_c", bufs=3, align_bytes=64)
                 nc.vector.quantize_mx(out=y_c[:].bitcast(FP8X4), scales=y_s[:, g, mc], in_=y_bf[:])
                 nc.sync.dma_start(

@@ -25,14 +25,14 @@ SLICES = GROUPS * PACK
 HALF = 512
 CH = 256
 NCH = M // CH
-V_ADD = ()
+V_ADD = (2,4,6)
 G_WEAVE = ()
 V_WEAVE = (7,)
 SPLIT = 80
 SPLITS = (0,96)
 WHOLE = (True,False)
 HOLD = "y2"
-Z0_LATE = False
+Z0_LATE = True
 
 
 def tile_list_null_slot_features_kernel(
@@ -43,7 +43,7 @@ def tile_list_null_slot_features_kernel(
     with ExitStack() as ctx:
         keep = ctx.enter_context(tc.tile_pool(name="keep", bufs=1))
         ring = ctx.enter_context(tc.tile_pool(name="ring", bufs=2))
-        psum = ctx.enter_context(tc.psum_pool(name="psum", bufs=8))
+        psum = ctx.enter_context(tc.psum_pool(name="psum", bufs=6))
 
         def held(shape, dtype, name, tag=None):
             return keep.tile(shape, dtype, name=name, tag=tag or name, align_bytes=64)
@@ -65,28 +65,30 @@ def tile_list_null_slot_features_kernel(
         w2_s = held([P, H], U8, "w2_s")
         wgs_sb = held([P, S], F32, "wgs_sb")
         gain_sb = held([P, GROUPS, PACK], F32, "gain_sb")
-        pages = [held([P, T2], F32, "page%d" % i) for i in range(2)]
         x = [held([P, PACK, M], F32, "x%d" % b) for b in range(GROUPS)]
-        z_c = [held([P, M], I32, "z_c%d" % b) for b in range(GROUPS)]
-        z_s = [held([P, M], U8, "z_s%d" % b) for b in range(GROUPS)]
+        z_c = [None, held([P, M], I32, "z_c1")]
+        z_s = [None, held([P, M], U8, "z_s1")]
         y_s = held([P, GROUPS, M], U8, "y_s")
         cos_w = held([P, S], F32, "cos_w")
         amp = held([P, S], F32, "amp")
+        amp_v = held([P, S], F32, "amp_v")
         zero_in = held([P, 1], F32, "zero_in")
         zero = held([P, 1], F32, "zero")
 
-        def bank():
+        def bank(for_vector=False):
+            if for_vector:
+                return psum.tile([P, 512], F32, name="bank_v", bufs=2)
             return psum.tile([P, 512], F32, name="bank")
 
         def entries(lst, lo, hi):
             return lst[:, lo // 16:hi // 16]
 
         nc.vector.memset(zero_in[:], 0.0)
-        nc.vector.memset(w2_s_raw[:].bitcast(I32), 0)
+        nc.gpsimd.memset(w2_s_raw[:].bitcast(I32), 0)
         nc.vector.memset(tab_s[:].bitcast(I32), 0)
-        nc.vector.memset(w4_s_raw[:].rearrange("p a c -> p (a c)").bitcast(I32), 0)
+        nc.gpsimd.memset(w4_s_raw[:].rearrange("p a c -> p (a c)").bitcast(I32), 0)
+        pages = [held([P, T2], F32, "page0")]
         nc.vector.memset(pages[0][:], 0.0)
-        nc.vector.memset(pages[1][:], 0.0)
         nc.scalar.activation(zero[:], zero_in[:], ACT.Silu)
 
         def load_raw(w, b):
@@ -97,7 +99,7 @@ def tile_list_null_slot_features_kernel(
             )
             return raw
 
-        tab_s_in = ring.tile([P, T // 4], I32, name="tab_s_in", tag="h", align_bytes=64)
+        tab_s_in = held([P, T // 4], I32, "tab_s_in", "page1")
         nc.sync.dma_start(list1[:], offs)
         for q in range(4):
             nc.sync.dma_start(
@@ -118,6 +120,9 @@ def tile_list_null_slot_features_kernel(
         nc.sync.dma_start(out=gain_sb[:], in_=gain.rearrange("(b p i) -> p b i", p=P, i=PACK))
         for q in range(4):
             nc.vector.tensor_copy(tab_s[32 * q:32 * q + 4, :].bitcast(I32), tab_s_in[32 * q:32 * q + 4, :])
+
+        pages.append(held([P, T2], F32, "page1"))
+        nc.gpsimd.memset(pages[1][:], 0.0)
 
         nc.vector.tensor_copy(v_s[:], tab_s[:].indirect(list1[:]))
         for lo in range(0, S, HALF):
@@ -156,22 +161,33 @@ def tile_list_null_slot_features_kernel(
             if not WHOLE[i]:
                 quantise(w31_c[0], w31_s[0], w_bf0, i * GROUP + P, (i + 1) * GROUP)
 
-        def product(codes, scales, col, lo):
-            acc = bank()
+        def product(codes, scales, col, lo, for_vector=False):
+            acc = bank(for_vector)
             nc.tensor.matmul_mx(
                 out=acc[:], lhsT=codes[:, col:col + P].bitcast(FP8X4), lhsT_scale=scales[:, col:col + P],
                 rhs=v_w[:, lo:lo + HALF].bitcast(FP8X4), rhs_scale=v_s[:, lo:lo + HALF], start=True, stop=True,
             )
             return acc
 
+        def early_sum(s):
+            b, t = divmod(s, PACK)
+            th = x[(s - 2) // PACK][:, (s - 2) % PACK, :]
+            for lo in range(0, S, HALF):
+                gate = product(w31_c[b], w31_s[b], GROUP + t * P, lo)
+                nc.scalar.activation(th[:, lo:lo + HALF], gate[:], ACT.Tanh, bias=zero[:])
+                linear = product(w2_c, w2_s, s * P, lo, True)
+                nc.vector.tensor_tensor(amp_v[:, lo:lo + HALF], linear[:], th[:, lo:lo + HALF], ALU.add)
+
         def features(s):
             b, t = divmod(s, PACK)
             page = pages[s % 2]
-            th = ring.tile([P, S], F32, name="th", bufs=2)
-            cs = ring.tile([P, S], F32, name="cs", bufs=2)
+            th = None
+            if s not in V_ADD:
+                th = ring.tile([P, S], F32, name="th", bufs=2)
+            cs = ring.tile([P, S], F32, name="cs", bufs=3)
             y2 = None
-            if s > 0:
-                y2 = ring.tile([P, S], F32, name="y2", bufs=3)
+            if s > 0 and s not in V_ADD:
+                y2 = ring.tile([P, S], F32, name="y2", bufs=2)
             if s == SLICES - 1:
                 h = held([P, S], F32, "h", "late_w4")
             else:
@@ -181,39 +197,39 @@ def tile_list_null_slot_features_kernel(
                 for vc in halves:
                     phase = product(w31_c[b], w31_s[b], t * P, vc.start)
                     nc.scalar.activation(cs[:, vc], phase[:], ACT.Abs, bias=zero[:])
-                    nc.scalar.activation(cs[:, vc], cs[:, vc], ACT.Sin, scale=-1.0, bias=math.pi / 2)
+                nc.scalar.activation(cs[:], cs[:], ACT.Sin, scale=-1.0, bias=math.pi / 2)
+                for vc in halves:
                     gate = product(w31_c[b], w31_s[b], GROUP + t * P, vc.start)
                     nc.scalar.activation(th[:, vc], gate[:], ACT.Tanh, bias=zero[:])
                 nc.vector.tensor_tensor(cos_w[:], cs[:], wgs_sb[:], ALU.mult)
                 for vc in halves:
-                    nc.vector.tensor_tensor(amp[:, vc], product(w2_c, w2_s, s * P, vc.start)[:], th[:, vc], ALU.add)
-                for vc, eng in zip(halves, (nc.vector, nc.gpsimd)):
-                    eng.tensor_tensor(h[:, vc], amp[:, vc], cos_w[:, vc], ALU.mult)
-                    nc.vector.tensor_copy(page[:].indirect(entries(list2, vc.start, vc.stop)), h[:, vc])
+                    nc.vector.tensor_tensor(amp[:, vc], product(w2_c, w2_s, s * P, vc.start, True)[:], th[:, vc], ALU.add)
+                nc.vector.tensor_tensor(h[:], amp[:], cos_w[:], ALU.mult)
+                nc.vector.tensor_copy(page[:].indirect(list2[:]), h[:])
             else:
                 for vc in halves:
                     phase = product(w31_c[b], w31_s[b], t * P, vc.start)
                     nc.scalar.activation(cs[:, vc], phase[:], ACT.Abs, bias=zero[:])
                 nc.scalar.activation(cs[:], cs[:], ACT.Sin, scale=-1.0, bias=math.pi / 2)
-                for vc in halves:
+                for vc in halves if s not in V_ADD else ():
                     gate = product(w31_c[b], w31_s[b], GROUP + t * P, vc.start)
                     nc.scalar.activation(th[:, vc], gate[:], ACT.Tanh, bias=zero[:])
                     nc.scalar.copy(y2[:, vc], product(w2_c, w2_s, s * P, vc.start)[:])
             if s > 0:
                 nc.gpsimd.tensor_tensor(cos_w[:], cs[:], wgs_sb[:], ALU.mult)
-                nc.gpsimd.tensor_tensor(amp[:], th[:], y2[:], ALU.add)
-                nc.gpsimd.tensor_tensor(h[:], amp[:], cos_w[:], ALU.mult)
+                if s in V_ADD:
+                    nc.gpsimd.tensor_tensor(h[:], amp_v[:], cos_w[:], ALU.mult)
+                else:
+                    nc.gpsimd.tensor_tensor(amp[:], th[:], y2[:], ALU.add)
+                    nc.gpsimd.tensor_tensor(h[:], amp[:], cos_w[:], ALU.mult)
                 nc.vector.tensor_copy(page[:].indirect(list2[:]), h[:])
             return th, cs, y2
 
         z_planes = {}
 
-        def read_slots(s, width):
+        def read_slots(s, lo, hi):
             b, t = divmod(s, PACK)
-            for lo in range(0, M, width):
-                nc.vector.tensor_copy(
-                    x[b][:, t, lo:lo + width], pages[s % 2][:].indirect(entries(list3, lo, lo + width))
-                )
+            nc.vector.tensor_copy(x[b][:, t, lo:hi], pages[s % 2][:].indirect(entries(list3, lo, hi)))
 
         def join_jam(s, width, gx):
             b, t = divmod(s, PACK)
@@ -226,6 +242,7 @@ def tile_list_null_slot_features_kernel(
             for lo in range(0, M, width):
                 mc = slice(lo, lo + width)
                 if gx is None:
+                    read_slots(s, lo, lo + width)
                     nc.vector.scalar_tensor_tensor(
                         out=z_planes[b][:, t, mc], in0=x[b][:, t, mc], scalar=gain_sb[:, b, t:t + 1],
                         in1=jam_sb[:, mc], op0=ALU.mult, op1=ALU.add,
@@ -244,11 +261,29 @@ def tile_list_null_slot_features_kernel(
             else:
                 nc.scalar.copy(dst, src)
 
+        def deal_w4(a):
+            nc.vector.tensor_copy(
+                w4_c[a][:].bitcast(U16).rearrange("p (g t q) -> p g q t", t=PACK, q=P),
+                w4_raw[:, a, :].bitcast(U16).rearrange("p (g q t) -> p g q t", t=PACK, q=P),
+            )
+            nc.vector.tensor_copy(
+                w4_s[a].rearrange("p (g t q) -> p g q t", t=PACK, q=P),
+                w4_s_raw[:, a, :].rearrange("p (g q t) -> p g q t", t=PACK, q=P),
+            )
+
+        w4_c, w4_s = {}, {}
         for s in range(SLICES):
             th, cs, y2 = features(s)
-            read_slots(s, CH if s == SLICES - 1 else M)
-            if s >= 2:
-                join_jam(s - 2, M, y2 if (HOLD == "y2" and y2 is not None) else cs)
+            if s == 1 + 0:
+                for i, raw in enumerate((w3_raw1, w1_raw1)):
+                    round_weight(raw, w_bf1[:, i * GROUP * PACK:(i + 1) * GROUP * PACK], nc.scalar.copy, 0, P)
+                quantise(w31_c[1], w31_s[1], w_bf1, 0, 2 * GROUP)
+            if s + 2 in V_ADD:
+                early_sum(s + 2)
+            if s < SLICES - 1:
+                read_slots(s, 0, M)
+            if s >= 3:
+                join_jam(s - 3, M, y2 if (HOLD == "y2" and y2 is not None) else cs)
             if s == 0:
                 w3_raw1 = load_raw(w3, 1)
                 w1_raw1 = load_raw(w1, 1)
@@ -260,31 +295,24 @@ def tile_list_null_slot_features_kernel(
                         out=w4_s_raw[32 * q:32 * q + 4, :, :].bitcast(I32),
                         in_=w4_scales[:, 4 * q:4 * q + 4, :].rearrange("a r c -> r a c").bitcast(I32),
                     )
-            if s == 2:
-                for i, raw in enumerate((w3_raw1, w1_raw1)):
-                    round_weight(raw, w_bf1[:, i * GROUP * PACK:(i + 1) * GROUP * PACK], nc.scalar.copy, 0, P)
-                quantise(w31_c[1], w31_s[1], w_bf1, 0, 2 * GROUP)
-            if s == 5:
+            if s == 6:
                 z0_bf = held([P, M * PACK], BF16, "z0_bf", "tab_w")
                 for c in range(4):
                     weave(z0_bf[:, c * M:(c + 1) * M], z_planes[0][:, :, c * 256:(c + 1) * 256], "s")
                 if not Z0_LATE:
                     quantise(z_c[0], z_s[0], z0_bf, 0, M)
 
-        join_jam(6, M, amp)
+        join_jam(5, M, cos_w)
+        join_jam(6, M, amp_v if 7 in V_ADD else amp)
+        late = held([P, 6 * H + 5 * M], U8, "late", "late_w4")
+        for a in range(GROUPS):
+            w4_c[a], w4_s[a] = late[:, 3 * a * H:(3 * a + 2) * H], late[:, (3 * a + 2) * H:(3 * a + 3) * H]
+        z_c[0] = late[:, 6 * H:6 * H + 4 * M].bitcast(I32)
+        z_s[0] = late[:, 6 * H + 4 * M:6 * H + 5 * M]
+        deal_w4(0)
+        quantise(z_c[0], z_s[0], z0_bf, 0, M)
         join_jam(7, CH, None)
-        w4_cs = held([P, 3 * GROUPS * H], U8, "w4_cs", "late_w4")
-        w4_c = w4_cs[:, 0:2 * GROUPS * H].rearrange("p (a c) -> p a c", a=GROUPS)
-        w4_s = w4_cs[:, 2 * GROUPS * H:3 * GROUPS * H].rearrange("p (a c) -> p a c", a=GROUPS)
-        for g in range(GROUPS):
-            nc.vector.tensor_copy(
-                w4_c[:, :, 2 * g * GROUP:2 * (g + 1) * GROUP].bitcast(U16).rearrange("p a (t q) -> p a q t", t=PACK),
-                w4_raw[:, :, 2 * g * GROUP:2 * (g + 1) * GROUP].bitcast(U16).rearrange("p a (q t) -> p a q t", t=PACK),
-            )
-            nc.vector.tensor_copy(
-                w4_s[:, :, g * GROUP:(g + 1) * GROUP].rearrange("p a (t q) -> p a q t", t=PACK),
-                w4_s_raw[:, :, g * GROUP:(g + 1) * GROUP].rearrange("p a (q t) -> p a q t", t=PACK),
-            )
+        deal_w4(1)
         for c in range(NCH):
             z_bf = ring.tile([P, CH * PACK], BF16, name="z_bf", bufs=4, align_bytes=64)
             weave(z_bf[:], z_planes[1][:, :, c * CH:(c + 1) * CH], "s")
@@ -296,16 +324,16 @@ def tile_list_null_slot_features_kernel(
             for g in range(GROUPS):
                 y = ring.tile([P, PACK, CH], F32, name="y", tag="jam_sb", bufs=4)
                 for pair in range(2):
-                    acc = bank()
-                    for e in range(2):
-                        col = g * GROUP + (2 * pair + e) * P
-                        for a in range(GROUPS):
+                    acc = bank(g == 1 and pair == 1)
+                    for a in range(GROUPS):
+                        for e in range(2):
+                            col = g * GROUP + (2 * pair + e) * P
                             nc.tensor.matmul_mx(
                                 out=acc[:, e * CH:(e + 1) * CH],
-                                lhsT=w4_c[:, a, 2 * col:2 * (col + P)].bitcast(FP4X4),
-                                lhsT_scale=w4_s[:, a, col:col + P],
+                                lhsT=w4_c[a][:, 2 * col:2 * (col + P)].bitcast(FP4X4),
+                                lhsT_scale=w4_s[a][:, col:col + P],
                                 rhs=z_c[a][:, mc].bitcast(FP8X4), rhs_scale=z_s[a][:, mc],
-                                start=(a == 0), stop=(a == GROUPS - 1),
+                                start=(a == 0 and e == 0), stop=(a == GROUPS - 1 and e == 1),
                             )
                     nc.vector.tensor_tensor(
                         y[:, 2 * pair:2 * pair + 2, :],

@@ -22,17 +22,13 @@ PACK = 4
 GROUP = P * PACK
 GROUPS = H // GROUP
 SLICES = GROUPS * PACK
-HALF = 512
-CH = 256
-NCH = M // CH
-V_ADD = (2,4,6)
-G_WEAVE = ()
-V_WEAVE = (7,)
-SPLIT = 80
-SPLITS = (0,96)
-WHOLE = (True,False)
-HOLD = "y2"
-Z0_LATE = True
+LAST = SLICES - 1
+BANK = 512
+CHUNK = 256
+CHUNKS = M // CHUNK
+PAGES = 2
+JAM_LAG = 3
+VECTOR_SUMS = (3, 6)
 
 
 def tile_list_null_slot_features_kernel(
@@ -48,6 +44,14 @@ def tile_list_null_slot_features_kernel(
         def held(shape, dtype, name, tag=None):
             return keep.tile(shape, dtype, name=name, tag=tag or name, align_bytes=64)
 
+        def bank(spare=False):
+            if spare:
+                return psum.tile([P, BANK], F32, name="spare_bank", bufs=2)
+            return psum.tile([P, BANK], F32, name="bank")
+
+        def entries(offsets, lo, hi):
+            return offsets[:, lo // 16:hi // 16]
+
         list1 = keep.tile([P, S // 16], U16, name="list1")
         list2 = keep.tile([P, S // 16], U16, name="list2")
         list3 = keep.tile([P, M // 16], U16, name="list3")
@@ -55,305 +59,273 @@ def tile_list_null_slot_features_kernel(
         tab_s = held([P, T], U8, "tab_s")
         v_w = held([P, S], U32, "v_w")
         v_s = held([P, S], U8, "v_s")
-        w2_s_raw = held([P, H], U8, "w2_s_raw")
-        w4_s_raw = held([P, GROUPS, H], U8, "w4_s_raw")
         w2_raw = held([P, H], I32, "w2_raw")
-        w4_raw = held([P, GROUPS, 2 * H], U8, "w4_raw")
-        w31_c = [held([P, 2 * GROUP], I32, "w31_c%d" % b) for b in range(GROUPS)]
-        w31_s = [held([P, 2 * GROUP], U8, "w31_s%d" % b) for b in range(GROUPS)]
+        w2_s_raw = held([P, H], U8, "w2_s_raw")
         w2_c = held([P, H], I32, "w2_c")
         w2_s = held([P, H], U8, "w2_s")
+        w4_raw = held([P, GROUPS, 2 * H], U8, "w4_raw")
+        w4_s_raw = held([P, H], U8, "w4_s_raw")
+        w31_c = [held([P, 2 * GROUP], I32, "w31_c%d" % g) for g in range(GROUPS)]
+        w31_s = [held([P, 2 * GROUP], U8, "w31_s%d" % g) for g in range(GROUPS)]
         wgs_sb = held([P, S], F32, "wgs_sb")
         gain_sb = held([P, GROUPS, PACK], F32, "gain_sb")
-        x = [held([P, PACK, M], F32, "x%d" % b) for b in range(GROUPS)]
-        z_c = [None, held([P, M], I32, "z_c1")]
-        z_s = [None, held([P, M], U8, "z_s1")]
-        y_s = held([P, GROUPS, M], U8, "y_s")
+        x = [held([P, PACK, M], F32, "x%d" % g) for g in range(GROUPS)]
         cos_w = held([P, S], F32, "cos_w")
         amp = held([P, S], F32, "amp")
-        amp_v = held([P, S], F32, "amp_v")
+        amp_early = held([P, S], F32, "amp_early")
+        y_s = held([P, GROUPS, M], U8, "y_s")
         zero_in = held([P, 1], F32, "zero_in")
         zero = held([P, 1], F32, "zero")
 
-        def bank(for_vector=False):
-            if for_vector:
-                return psum.tile([P, 512], F32, name="bank_v", bufs=2)
-            return psum.tile([P, 512], F32, name="bank")
-
-        def entries(lst, lo, hi):
-            return lst[:, lo // 16:hi // 16]
+        def x_slice(s):
+            return x[s // PACK][:, s % PACK, :]
 
         nc.vector.memset(zero_in[:], 0.0)
         nc.gpsimd.memset(w2_s_raw[:].bitcast(I32), 0)
         nc.vector.memset(tab_s[:].bitcast(I32), 0)
-        nc.gpsimd.memset(w4_s_raw[:].rearrange("p a c -> p (a c)").bitcast(I32), 0)
+        nc.gpsimd.memset(w4_s_raw[:].bitcast(I32), 0)
         pages = [held([P, T2], F32, "page0")]
         nc.vector.memset(pages[0][:], 0.0)
         nc.scalar.activation(zero[:], zero_in[:], ACT.Silu)
 
-        def load_raw(w, b):
+        def load_weight(w, g):
             raw = ring.tile([P, PACK, GROUP], F32, name="w_raw")
             nc.sync.dma_start(
-                out=raw[:],
-                in_=w[:, b * GROUP:(b + 1) * GROUP].rearrange("(p j) c -> p j c", j=PACK),
+                out=raw[:], in_=w[:, g * GROUP:(g + 1) * GROUP].rearrange("(p j) c -> p j c", j=PACK)
             )
             return raw
 
+        def load_scale_rows(tile, rows):
+            for q in range(4):
+                nc.sync.dma_start(out=tile[32 * q:32 * q + 4, :], in_=rows[4 * q:4 * q + 4, :].bitcast(I32))
+
         tab_s_in = held([P, T // 4], I32, "tab_s_in", "page1")
         nc.sync.dma_start(list1[:], offs)
-        for q in range(4):
-            nc.sync.dma_start(
-                out=tab_s_in[32 * q:32 * q + 4, :], in_=tab_scales[0, 4 * q:4 * q + 4, :].bitcast(I32)
-            )
-        w3_raw0 = load_raw(w3, 0)
+        load_scale_rows(tab_s_in, tab_scales[0])
+        w3_raw = load_weight(w3, 0)
         nc.sync.dma_start(out=tab_w[:], in_=tab_words[0].rearrange("p t i -> p (t i)").bitcast(I32))
-        w1_raw0 = load_raw(w1, 0)
-        for q in range(4):
-            nc.sync.dma_start(
-                out=w2_s_raw[32 * q:32 * q + 4, :].bitcast(I32), in_=w2_scales[0, 4 * q:4 * q + 4, :].bitcast(I32)
-            )
+        w1_raw = load_weight(w1, 0)
+        load_scale_rows(w2_s_raw[:].bitcast(I32), w2_scales[0])
         nc.sync.dma_start(out=w2_raw[:], in_=w2_words[0].rearrange("p c i -> p (c i)").bitcast(I32))
-        nc.sync.dma_start(out=wgs_sb[:, 0:HALF], in_=wgs[:, 0:HALF])
+        nc.sync.dma_start(out=wgs_sb[:], in_=wgs)
         nc.sync.dma_start(list2[:], offs2)
-        nc.sync.dma_start(out=wgs_sb[:, HALF:S], in_=wgs[:, HALF:S])
         nc.sync.dma_start(list3[:], offs3)
-        nc.sync.dma_start(out=gain_sb[:], in_=gain.rearrange("(b p i) -> p b i", p=P, i=PACK))
+        nc.sync.dma_start(out=gain_sb[:], in_=gain.rearrange("(g p t) -> p g t", p=P, t=PACK))
         for q in range(4):
             nc.vector.tensor_copy(tab_s[32 * q:32 * q + 4, :].bitcast(I32), tab_s_in[32 * q:32 * q + 4, :])
-
         pages.append(held([P, T2], F32, "page1"))
         nc.gpsimd.memset(pages[1][:], 0.0)
 
         nc.vector.tensor_copy(v_s[:], tab_s[:].indirect(list1[:]))
-        for lo in range(0, S, HALF):
+        for lo in range(0, S, BANK):
             nc.vector.tensor_copy(
-                v_w[:, lo:lo + HALF], tab_w[:].bitcast(U32).indirect(entries(list1, lo, lo + HALF))
+                v_w[:, lo:lo + BANK], tab_w[:].bitcast(U32).indirect(entries(list1, lo, lo + BANK))
             )
 
-        def round_weight(raw, grouped, copy, lo, hi):
+        def round_weight(copy, rounded, raw, places=slice(0, PACK)):
             copy(
-                grouped.rearrange("p (t m j) -> p m j t", t=PACK, j=PACK)[:, lo:hi],
-                raw[:].rearrange("p j (m t) -> p m j t", t=PACK)[:, lo:hi],
+                rounded.rearrange("p (t q j) -> p q j t", t=PACK, j=PACK)[:, :, :, places],
+                raw[:].rearrange("p j (q t) -> p q j t", t=PACK)[:, :, :, places],
             )
 
-        def quantise(codes, scales, grouped, lo, hi):
+        def quantise(codes, scales, rounded, lo, hi):
             nc.vector.quantize_mx(
-                out=codes[:, lo:hi].bitcast(FP8X4), scales=scales[:, lo:hi], in_=grouped[:, PACK * lo:PACK * hi]
+                out=codes[:, lo:hi].bitcast(FP8X4), scales=scales[:, lo:hi], in_=rounded[:, PACK * lo:PACK * hi]
+            )
+
+        def deal(dealt, raw):
+            nc.vector.tensor_copy(
+                dealt.rearrange("p (g t q) -> p g q t", t=PACK, q=P), raw.rearrange("p (g q t) -> p g q t", t=PACK, q=P)
             )
 
         w_bf = x[1][:].rearrange("p t m -> p (t m)").bitcast(BF16)
-        w_bf0, w_bf1 = w_bf[:, 0:2 * GROUP * PACK], w_bf[:, 2 * GROUP * PACK:4 * GROUP * PACK]
-        for i, raw in enumerate((w3_raw0, w1_raw0)):
-            part = w_bf0[:, i * GROUP * PACK:(i + 1) * GROUP * PACK]
-            if SPLITS[i] > 0:
-                round_weight(raw, part, nc.vector.tensor_copy, 0, SPLITS[i])
-            round_weight(raw, part, nc.scalar.copy, SPLITS[i], P)
-            quantise(w31_c[0], w31_s[0], w_bf0, i * GROUP, i * GROUP + (GROUP if WHOLE[i] else P))
-        nc.vector.tensor_copy(
-            w2_s[:].rearrange("p (g t q) -> p g q t", t=PACK, q=P),
-            w2_s_raw[:].rearrange("p (g q t) -> p g q t", t=PACK, q=P),
-        )
-        nc.vector.tensor_copy(
-            w2_c[:].rearrange("p (g t q) -> p g q t", t=PACK, q=P),
-            w2_raw[:].rearrange("p (g q t) -> p g q t", t=PACK, q=P),
-        )
-        for i in range(2):
-            if not WHOLE[i]:
-                quantise(w31_c[0], w31_s[0], w_bf0, i * GROUP + P, (i + 1) * GROUP)
+        w31_bf = [w_bf[:, 2 * g * GROUP * PACK:2 * (g + 1) * GROUP * PACK] for g in range(GROUPS)]
+        w3_part, w1_part = slice(0, GROUP * PACK), slice(GROUP * PACK, 2 * GROUP * PACK)
+        round_weight(nc.scalar.copy, w31_bf[0][:, w3_part], w3_raw)
+        quantise(w31_c[0], w31_s[0], w31_bf[0], 0, GROUP)
+        round_weight(nc.vector.tensor_copy, w31_bf[0][:, w1_part], w1_raw, slice(0, 1))
+        quantise(w31_c[0], w31_s[0], w31_bf[0], GROUP, GROUP + P)
+        round_weight(nc.vector.tensor_copy, w31_bf[0][:, w1_part], w1_raw, slice(1, PACK))
+        deal(w2_s[:], w2_s_raw[:])
+        deal(w2_c[:], w2_raw[:])
+        quantise(w31_c[0], w31_s[0], w31_bf[0], GROUP + P, 2 * GROUP)
 
-        def product(codes, scales, col, lo, for_vector=False):
-            acc = bank(for_vector)
+        def product(codes, scales, col, lo, spare=False):
+            acc = bank(spare)
             nc.tensor.matmul_mx(
                 out=acc[:], lhsT=codes[:, col:col + P].bitcast(FP8X4), lhsT_scale=scales[:, col:col + P],
-                rhs=v_w[:, lo:lo + HALF].bitcast(FP8X4), rhs_scale=v_s[:, lo:lo + HALF], start=True, stop=True,
+                rhs=v_w[:, lo:lo + BANK].bitcast(FP8X4), rhs_scale=v_s[:, lo:lo + BANK], start=True, stop=True,
             )
             return acc
 
-        def early_sum(s):
-            b, t = divmod(s, PACK)
-            th = x[(s - 2) // PACK][:, (s - 2) % PACK, :]
-            for lo in range(0, S, HALF):
-                gate = product(w31_c[b], w31_s[b], GROUP + t * P, lo)
-                nc.scalar.activation(th[:, lo:lo + HALF], gate[:], ACT.Tanh, bias=zero[:])
-                linear = product(w2_c, w2_s, s * P, lo, True)
-                nc.vector.tensor_tensor(amp_v[:, lo:lo + HALF], linear[:], th[:, lo:lo + HALF], ALU.add)
+        def cosine(s):
+            cos = ring.tile([P, S], F32, name="cos", bufs=3)
+            for lo in range(0, S, BANK):
+                y3 = product(w31_c[s // PACK], w31_s[s // PACK], s % PACK * P, lo)
+                nc.scalar.activation(cos[:, lo:lo + BANK], y3[:], ACT.Abs, bias=zero[:])
+            nc.scalar.activation(cos[:], cos[:], ACT.Sin, scale=-1.0, bias=math.pi / 2)
+            return cos
 
-        def features(s):
-            b, t = divmod(s, PACK)
-            page = pages[s % 2]
-            th = None
-            if s not in V_ADD:
-                th = ring.tile([P, S], F32, name="th", bufs=2)
-            cs = ring.tile([P, S], F32, name="cs", bufs=3)
-            y2 = None
-            if s > 0 and s not in V_ADD:
-                y2 = ring.tile([P, S], F32, name="y2", bufs=2)
-            if s == SLICES - 1:
-                h = held([P, S], F32, "h", "late_w4")
-            else:
-                h = ring.tile([P, S], F32, name="h", align_bytes=64)
-            halves = [slice(lo, lo + HALF) for lo in range(0, S, HALF)]
+        def tanh_half(tanh, s, lo):
+            y1 = product(w31_c[s // PACK], w31_s[s // PACK], GROUP + s % PACK * P, lo)
+            nc.scalar.activation(tanh[:, lo:lo + BANK], y1[:], ACT.Tanh, bias=zero[:])
+
+        def sum_on_vector(out, tanh, s):
+            for lo in range(0, S, BANK):
+                tanh_half(tanh, s, lo)
+                y2 = product(w2_c, w2_s, s * P, lo, spare=True)
+                nc.vector.tensor_tensor(out[:, lo:lo + BANK], y2[:], tanh[:, lo:lo + BANK], ALU.add)
+
+        def features(s, h):
+            cos = cosine(s)
             if s == 0:
-                for vc in halves:
-                    phase = product(w31_c[b], w31_s[b], t * P, vc.start)
-                    nc.scalar.activation(cs[:, vc], phase[:], ACT.Abs, bias=zero[:])
-                nc.scalar.activation(cs[:], cs[:], ACT.Sin, scale=-1.0, bias=math.pi / 2)
-                for vc in halves:
-                    gate = product(w31_c[b], w31_s[b], GROUP + t * P, vc.start)
-                    nc.scalar.activation(th[:, vc], gate[:], ACT.Tanh, bias=zero[:])
-                nc.vector.tensor_tensor(cos_w[:], cs[:], wgs_sb[:], ALU.mult)
-                for vc in halves:
-                    nc.vector.tensor_tensor(amp[:, vc], product(w2_c, w2_s, s * P, vc.start, True)[:], th[:, vc], ALU.add)
+                tanh = ring.tile([P, S], F32, name="tanh")
+                nc.vector.tensor_tensor(cos_w[:], cos[:], wgs_sb[:], ALU.mult)
+                sum_on_vector(amp, tanh, s)
                 nc.vector.tensor_tensor(h[:], amp[:], cos_w[:], ALU.mult)
-                nc.vector.tensor_copy(page[:].indirect(list2[:]), h[:])
+                spent = cos
+            elif s in VECTOR_SUMS:
+                nc.gpsimd.tensor_tensor(cos_w[:], cos[:], wgs_sb[:], ALU.mult)
+                nc.gpsimd.tensor_tensor(h[:], amp_early[:], cos_w[:], ALU.mult)
+                spent = cos
             else:
-                for vc in halves:
-                    phase = product(w31_c[b], w31_s[b], t * P, vc.start)
-                    nc.scalar.activation(cs[:, vc], phase[:], ACT.Abs, bias=zero[:])
-                nc.scalar.activation(cs[:], cs[:], ACT.Sin, scale=-1.0, bias=math.pi / 2)
-                for vc in halves if s not in V_ADD else ():
-                    gate = product(w31_c[b], w31_s[b], GROUP + t * P, vc.start)
-                    nc.scalar.activation(th[:, vc], gate[:], ACT.Tanh, bias=zero[:])
-                    nc.scalar.copy(y2[:, vc], product(w2_c, w2_s, s * P, vc.start)[:])
-            if s > 0:
-                nc.gpsimd.tensor_tensor(cos_w[:], cs[:], wgs_sb[:], ALU.mult)
-                if s in V_ADD:
-                    nc.gpsimd.tensor_tensor(h[:], amp_v[:], cos_w[:], ALU.mult)
-                else:
-                    nc.gpsimd.tensor_tensor(amp[:], th[:], y2[:], ALU.add)
-                    nc.gpsimd.tensor_tensor(h[:], amp[:], cos_w[:], ALU.mult)
-                nc.vector.tensor_copy(page[:].indirect(list2[:]), h[:])
-            return th, cs, y2
-
-        z_planes = {}
+                tanh = ring.tile([P, S], F32, name="tanh")
+                y2_sb = ring.tile([P, S], F32, name="y2_sb")
+                for lo in range(0, S, BANK):
+                    tanh_half(tanh, s, lo)
+                    nc.scalar.copy(y2_sb[:, lo:lo + BANK], product(w2_c, w2_s, s * P, lo)[:])
+                nc.gpsimd.tensor_tensor(cos_w[:], cos[:], wgs_sb[:], ALU.mult)
+                nc.gpsimd.tensor_tensor(amp[:], tanh[:], y2_sb[:], ALU.add)
+                nc.gpsimd.tensor_tensor(h[:], amp[:], cos_w[:], ALU.mult)
+                spent = y2_sb
+            nc.vector.tensor_copy(pages[s % PAGES][:].indirect(list2[:]), h[:])
+            return spent
 
         def read_slots(s, lo, hi):
-            b, t = divmod(s, PACK)
-            nc.vector.tensor_copy(x[b][:, t, lo:hi], pages[s % 2][:].indirect(entries(list3, lo, hi)))
+            nc.vector.tensor_copy(x_slice(s)[:, lo:hi], pages[s % PAGES][:].indirect(entries(list3, lo, hi)))
 
-        def join_jam(s, width, gx):
-            b, t = divmod(s, PACK)
+        z_slices = {}
+
+        def load_jam(s):
+            g, t = divmod(s, PACK)
             if t == 0:
-                z_planes[b] = held([P, PACK, M], BF16, "z_planes")
-            jam_sb = ring.tile([P, M], F32, name="jam_sb", bufs=4)
+                z_slices[g] = held([P, PACK, M], BF16, "z_slices")
+            rows = ring.tile([P, M], F32, name="jam_sb", bufs=4)
             nc.sync.dma_start(
-                out=jam_sb[:], in_=jam[b * GROUP:(b + 1) * GROUP, :].rearrange("(p t) m -> p t m", t=PACK)[:, t, :]
+                out=rows[:], in_=jam[g * GROUP:(g + 1) * GROUP, :].rearrange("(p t) m -> p t m", t=PACK)[:, t, :]
             )
-            for lo in range(0, M, width):
-                mc = slice(lo, lo + width)
-                if gx is None:
-                    read_slots(s, lo, lo + width)
-                    nc.vector.scalar_tensor_tensor(
-                        out=z_planes[b][:, t, mc], in0=x[b][:, t, mc], scalar=gain_sb[:, b, t:t + 1],
-                        in1=jam_sb[:, mc], op0=ALU.mult, op1=ALU.add,
-                    )
-                else:
-                    nc.scalar.activation(gx[:, mc], x[b][:, t, mc], ACT.Copy, scale=gain_sb[:, b, t:t + 1])
-                    nc.gpsimd.tensor_tensor(z_planes[b][:, t, mc], gx[:, mc], jam_sb[:, mc], ALU.add)
+            return rows
 
-        def weave(dst, src, eng):
-            dst = dst.rearrange("p (c i t) -> p c t i", i=4, t=PACK)
-            src = src.rearrange("p t (c i) -> p c t i", i=4)
-            if eng == "g":
-                nc.gpsimd.tensor_scalar(dst, src, 1.0, 0.0, ALU.mult, ALU.add)
-            elif eng == "v":
-                nc.vector.tensor_copy(dst, src)
-            else:
-                nc.scalar.copy(dst, src)
+        def join_jam(s, gain_x):
+            g, t = divmod(s, PACK)
+            rows = load_jam(s)
+            nc.scalar.activation(gain_x, x_slice(s), ACT.Copy, scale=gain_sb[:, g, t:t + 1])
+            nc.gpsimd.tensor_tensor(z_slices[g][:, t, :], gain_x, rows[:], ALU.add)
 
-        def deal_w4(a):
-            nc.vector.tensor_copy(
-                w4_c[a][:].bitcast(U16).rearrange("p (g t q) -> p g q t", t=PACK, q=P),
-                w4_raw[:, a, :].bitcast(U16).rearrange("p (g q t) -> p g q t", t=PACK, q=P),
-            )
-            nc.vector.tensor_copy(
-                w4_s[a].rearrange("p (g t q) -> p g q t", t=PACK, q=P),
-                w4_s_raw[:, a, :].rearrange("p (g q t) -> p g q t", t=PACK, q=P),
+        def weave(copy, woven, slices):
+            copy(
+                woven.rearrange("p (c i t) -> p c t i", i=4, t=PACK), slices.rearrange("p t (c i) -> p c t i", i=4)
             )
 
-        w4_c, w4_s = {}, {}
         for s in range(SLICES):
-            th, cs, y2 = features(s)
-            if s == 1 + 0:
-                for i, raw in enumerate((w3_raw1, w1_raw1)):
-                    round_weight(raw, w_bf1[:, i * GROUP * PACK:(i + 1) * GROUP * PACK], nc.scalar.copy, 0, P)
-                quantise(w31_c[1], w31_s[1], w_bf1, 0, 2 * GROUP)
-            if s + 2 in V_ADD:
-                early_sum(s + 2)
-            if s < SLICES - 1:
+            if s == LAST:
+                h = held([P, S], F32, "h", "late")
+            else:
+                h = ring.tile([P, S], F32, name="h")
+            spent = features(s, h)
+            if s == 1:
+                round_weight(nc.scalar.copy, w31_bf[1][:, w3_part], w3_raw)
+                round_weight(nc.scalar.copy, w31_bf[1][:, w1_part], w1_raw)
+                quantise(w31_c[1], w31_s[1], w31_bf[1], 0, 2 * GROUP)
+            if s + 2 in VECTOR_SUMS:
+                sum_on_vector(amp_early, x_slice(s), s + 2)
+            if s < LAST:
                 read_slots(s, 0, M)
-            if s >= 3:
-                join_jam(s - 3, M, y2 if (HOLD == "y2" and y2 is not None) else cs)
+            if s >= JAM_LAG:
+                join_jam(s - JAM_LAG, spent[:])
             if s == 0:
-                w3_raw1 = load_raw(w3, 1)
-                w1_raw1 = load_raw(w1, 1)
+                w3_raw = load_weight(w3, 1)
+                w1_raw = load_weight(w1, 1)
                 nc.sync.dma_start(
                     out=w4_raw[:].bitcast(I32), in_=w4_words.rearrange("a p c -> p a c").bitcast(I32)
                 )
                 for q in range(4):
                     nc.sync.dma_start(
-                        out=w4_s_raw[32 * q:32 * q + 4, :, :].bitcast(I32),
-                        in_=w4_scales[:, 4 * q:4 * q + 4, :].rearrange("a r c -> r a c").bitcast(I32),
+                        out=w4_s_raw[32 * q:32 * q + 4 * GROUPS, :].bitcast(I32),
+                        in_=w4_scales[:, 4 * q:4 * q + 4, :].bitcast(I32),
                     )
-            if s == 6:
+            if s == PACK - 1 + JAM_LAG:
                 z0_bf = held([P, M * PACK], BF16, "z0_bf", "tab_w")
-                for c in range(4):
-                    weave(z0_bf[:, c * M:(c + 1) * M], z_planes[0][:, :, c * 256:(c + 1) * 256], "s")
-                if not Z0_LATE:
-                    quantise(z_c[0], z_s[0], z0_bf, 0, M)
+                for lo in range(0, M, CHUNK):
+                    weave(nc.scalar.copy, z0_bf[:, PACK * lo:PACK * (lo + CHUNK)], z_slices[0][:, :, lo:lo + CHUNK])
 
-        join_jam(5, M, cos_w)
-        join_jam(6, M, amp_v if 7 in V_ADD else amp)
-        late = held([P, 6 * H + 5 * M], U8, "late", "late_w4")
-        for a in range(GROUPS):
-            w4_c[a], w4_s[a] = late[:, 3 * a * H:(3 * a + 2) * H], late[:, (3 * a + 2) * H:(3 * a + 3) * H]
-        z_c[0] = late[:, 6 * H:6 * H + 4 * M].bitcast(I32)
-        z_s[0] = late[:, 6 * H + 4 * M:6 * H + 5 * M]
-        deal_w4(0)
-        quantise(z_c[0], z_s[0], z0_bf, 0, M)
-        join_jam(7, CH, None)
-        deal_w4(1)
-        for c in range(NCH):
-            z_bf = ring.tile([P, CH * PACK], BF16, name="z_bf", bufs=4, align_bytes=64)
-            weave(z_bf[:], z_planes[1][:, :, c * CH:(c + 1) * CH], "s")
-            nc.vector.quantize_mx(
-                out=z_c[1][:, c * CH:(c + 1) * CH].bitcast(FP8X4), scales=z_s[1][:, c * CH:(c + 1) * CH], in_=z_bf[:]
+        join_jam(LAST - 2, cos_w[:])
+        join_jam(LAST - 1, amp[:])
+
+        late = held([P, 2 * GROUPS * H + 5 * M + H], U8, "late")
+        w4_c = [late[:, 2 * a * H:2 * (a + 1) * H] for a in range(GROUPS)]
+        z_c = [late[:, 4 * H:4 * H + 4 * M].bitcast(I32), held([P, M], I32, "z_c1")]
+        z_s = [late[:, 4 * H + 4 * M:4 * H + 5 * M], held([P, M], U8, "z_s1")]
+        w4_s = [late[:, 4 * H + 5 * M:5 * H + 5 * M], held([P, H], U8, "w4_s1")]
+        rows = load_jam(LAST)
+        read_slots(LAST, 0, M)
+        deal(w4_s[0], w4_s_raw[:])
+        for q in range(4):
+            nc.sync.dma_start(
+                out=w4_s[1][32 * q:32 * q + 4, :].bitcast(I32), in_=w4_s[0][32 * q + 4:32 * q + 8, :].bitcast(I32)
             )
-        for c in range(NCH):
-            mc = slice(c * CH, (c + 1) * CH)
+        deal(w4_c[0].bitcast(U16), w4_raw[:, 0, :].bitcast(U16))
+        quantise(z_c[0], z_s[0], z0_bf, 0, M // 2)
+        for lo in range(0, M, CHUNK):
+            nc.vector.scalar_tensor_tensor(
+                out=z_slices[1][:, PACK - 1, lo:lo + CHUNK], in0=x_slice(LAST)[:, lo:lo + CHUNK],
+                scalar=gain_sb[:, GROUPS - 1, PACK - 1:PACK], in1=rows[:, lo:lo + CHUNK], op0=ALU.mult, op1=ALU.add,
+            )
+        deal(w4_c[1].bitcast(U16), w4_raw[:, 1, :].bitcast(U16))
+        for lo in range(0, M, CHUNK):
+            z_bf = ring.tile([P, CHUNK * PACK], BF16, name="z_bf", bufs=CHUNKS, align_bytes=64)
+            weave(nc.scalar.copy, z_bf[:], z_slices[1][:, :, lo:lo + CHUNK])
+            nc.vector.quantize_mx(
+                out=z_c[1][:, lo:lo + CHUNK].bitcast(FP8X4), scales=z_s[1][:, lo:lo + CHUNK], in_=z_bf[:]
+            )
+            if lo == 0:
+                quantise(z_c[0], z_s[0], z0_bf, M // 2, M)
+
+        for lo in range(0, M, CHUNK):
+            cols = slice(lo, lo + CHUNK)
+            passes = (0, 1) if lo == 0 else (1, 0)
             for g in range(GROUPS):
-                y = ring.tile([P, PACK, CH], F32, name="y", tag="jam_sb", bufs=4)
+                if g == 0:
+                    y = ring.tile([P, PACK, CHUNK], F32, name="y", tag="cos", bufs=3)
+                else:
+                    y = ring.tile([P, PACK, CHUNK], F32, name="y", tag="jam_sb", bufs=4)
                 for pair in range(2):
-                    acc = bank(g == 1 and pair == 1)
-                    for a in range(GROUPS):
+                    acc = bank(spare=(g == 1 and pair == 1))
+                    for a in passes:
                         for e in range(2):
                             col = g * GROUP + (2 * pair + e) * P
                             nc.tensor.matmul_mx(
-                                out=acc[:, e * CH:(e + 1) * CH],
+                                out=acc[:, e * CHUNK:(e + 1) * CHUNK],
                                 lhsT=w4_c[a][:, 2 * col:2 * (col + P)].bitcast(FP4X4),
                                 lhsT_scale=w4_s[a][:, col:col + P],
-                                rhs=z_c[a][:, mc].bitcast(FP8X4), rhs_scale=z_s[a][:, mc],
-                                start=(a == 0 and e == 0), stop=(a == GROUPS - 1 and e == 1),
+                                rhs=z_c[a][:, cols].bitcast(FP8X4), rhs_scale=z_s[a][:, cols],
+                                start=(a == passes[0] and e == 0), stop=(a == passes[1] and e == 1),
                             )
                     nc.vector.tensor_tensor(
-                        y[:, 2 * pair:2 * pair + 2, :],
-                        acc[:].rearrange("p (e m) -> p e m", e=2),
-                        x[g][:, 2 * pair:2 * pair + 2, mc],
-                        ALU.add,
+                        y[:, 2 * pair:2 * pair + 2, :], acc[:].rearrange("p (e m) -> p e m", e=2),
+                        x[g][:, 2 * pair:2 * pair + 2, cols], ALU.add,
                     )
                 nc.sync.dma_start(
-                    out=out_0[g * GROUP:(g + 1) * GROUP, mc].rearrange("(p t) m -> p t m", t=PACK), in_=y[:]
+                    out=out_0[g * GROUP:(g + 1) * GROUP, cols].rearrange("(p t) m -> p t m", t=PACK), in_=y[:]
                 )
-                y_bf = ring.tile([P, CH * PACK], BF16, name="y_bf", bufs=3, align_bytes=64)
-                n = GROUPS * c + g
-                weave(y_bf[:], y[:], "g" if n in G_WEAVE else "v" if n in V_WEAVE else "s")
-                y_c = ring.tile([P, CH], I32, name="y_c", bufs=3, align_bytes=64)
-                nc.vector.quantize_mx(out=y_c[:].bitcast(FP8X4), scales=y_s[:, g, mc], in_=y_bf[:])
-                nc.sync.dma_start(
-                    out=out_1[g, :, mc, :].rearrange("p m t -> p (m t)").bitcast(I32), in_=y_c[:]
-                )
+                y_bf = ring.tile([P, CHUNK * PACK], BF16, name="y_bf", bufs=3, align_bytes=64)
+                very_last = lo + CHUNK == M and g == GROUPS - 1
+                weave(nc.vector.tensor_copy if very_last else nc.scalar.copy, y_bf[:], y[:])
+                y_c = ring.tile([P, CHUNK], I32, name="y_c", bufs=4, align_bytes=64)
+                nc.vector.quantize_mx(out=y_c[:].bitcast(FP8X4), scales=y_s[:, g, cols], in_=y_bf[:])
+                nc.sync.dma_start(out=out_1[g, :, cols, :].rearrange("p m t -> p (m t)").bitcast(I32), in_=y_c[:])
         for q in range(4):
-            nc.sync.dma_start(
+            nc.scalar.dma_start(
                 out=out_2[:, 4 * q:4 * q + 4, :].rearrange("g r m -> r g m").bitcast(I32),
                 in_=y_s[32 * q:32 * q + 4, :, :].bitcast(I32),
             )

import math
from contextlib import ExitStack

import concourse.mybir as mybir

K, T, S, H, T2, M = 512, 4096, 1024, 1024, 2048, 1024
FLOPS = 2 * (3 * K * H * S + H * H * M)

F32 = mybir.dt.float32
BF16 = mybir.dt.bfloat16
I32 = mybir.dt.int32
U32 = mybir.dt.uint32
U16 = mybir.dt.uint16
U8 = mybir.dt.uint8
FP8X4 = mybir.dt.float8_e4m3fn_x4
FP4X4 = mybir.dt.float4_e2m1fn_x4
ACT = mybir.ActivationFunctionType
ALU = mybir.AluOpType

P = 128
PACK = 4
GROUP = P * PACK
GROUPS = H // GROUP
SLICES = GROUPS * PACK
LAST = SLICES - 1
BANK = 512
CHUNK = 256
CHUNKS = M // CHUNK
PAGES = 2
JAM_LAG = 3
VECTOR_SUMS = (3, 6)


def tile_list_null_slot_features_kernel(
    tc, tab_words, tab_scales, offs, w1, w2_words, w2_scales, w3, wgs, offs2, offs3, gain, jam,
    w4_words, w4_scales, out_0, out_1, out_2,
):
    nc = tc.nc
    with ExitStack() as ctx:
        keep = ctx.enter_context(tc.tile_pool(name="keep", bufs=1))
        ring = ctx.enter_context(tc.tile_pool(name="ring", bufs=2))
        psum = ctx.enter_context(tc.psum_pool(name="psum", bufs=6))

        def held(shape, dtype, name, tag=None):
            return keep.tile(shape, dtype, name=name, tag=tag or name, align_bytes=64)

        def bank(spare=False):
            if spare:
                return psum.tile([P, BANK], F32, name="spare_bank", bufs=2)
            return psum.tile([P, BANK], F32, name="bank")

        def entries(offsets, lo, hi):
            return offsets[:, lo // 16:hi // 16]

        list1 = keep.tile([P, S // 16], U16, name="list1")
        list2 = keep.tile([P, S // 16], U16, name="list2")
        list3 = keep.tile([P, M // 16], U16, name="list3")
        tab_w = held([P, T], I32, "tab_w")
        tab_s = held([P, T], U8, "tab_s")
        v_w = held([P, S], U32, "v_w")
        v_s = held([P, S], U8, "v_s")
        w2_raw = held([P, H], I32, "w2_raw")
        w2_s_raw = held([P, H], U8, "w2_s_raw")
        w2_c = held([P, H], I32, "w2_c")
        w2_s = held([P, H], U8, "w2_s")
        w4_raw = held([P, GROUPS, 2 * H], U8, "w4_raw")
        w4_s_raw = held([P, H], U8, "w4_s_raw")
        w31_c = [held([P, 2 * GROUP], I32, "w31_c%d" % g) for g in range(GROUPS)]
        w31_s = [held([P, 2 * GROUP], U8, "w31_s%d" % g) for g in range(GROUPS)]
        wgs_sb = held([P, S], F32, "wgs_sb")
        gain_sb = held([P, GROUPS, PACK], F32, "gain_sb")
        x = [held([P, PACK, M], F32, "x%d" % g) for g in range(GROUPS)]
        cos_w = held([P, S], F32, "cos_w")
        amp = held([P, S], F32, "amp")
        amp_early = held([P, S], F32, "amp_early")
        y_s = held([P, GROUPS, M], U8, "y_s")
        zero_in = held([P, 1], F32, "zero_in")
        zero = held([P, 1], F32, "zero")

        def x_slice(s):
            return x[s // PACK][:, s % PACK, :]

        nc.vector.memset(zero_in[:], 0.0)
        nc.gpsimd.memset(w2_s_raw[:].bitcast(I32), 0)
        nc.vector.memset(tab_s[:].bitcast(I32), 0)
        nc.gpsimd.memset(w4_s_raw[:].bitcast(I32), 0)
        pages = [held([P, T2], F32, "page0")]
        nc.vector.memset(pages[0][:], 0.0)
        nc.scalar.activation(zero[:], zero_in[:], ACT.Silu)

        def load_weight(w, g):
            raw = ring.tile([P, PACK, GROUP], F32, name="w_raw")
            nc.sync.dma_start(
                out=raw[:], in_=w[:, g * GROUP:(g + 1) * GROUP].rearrange("(p j) c -> p j c", j=PACK)
            )
            return raw

        def load_scale_rows(tile, rows):
            for q in range(4):
                nc.sync.dma_start(out=tile[32 * q:32 * q + 4, :], in_=rows[4 * q:4 * q + 4, :].bitcast(I32))

        tab_s_in = held([P, T // 4], I32, "tab_s_in", "page1")
        nc.sync.dma_start(list1[:], offs)
        load_scale_rows(tab_s_in, tab_scales[0])
        w3_raw = load_weight(w3, 0)
        nc.sync.dma_start(out=tab_w[:], in_=tab_words[0].rearrange("p t i -> p (t i)").bitcast(I32))
        w1_raw = load_weight(w1, 0)
        load_scale_rows(w2_s_raw[:].bitcast(I32), w2_scales[0])
        nc.sync.dma_start(out=w2_raw[:], in_=w2_words[0].rearrange("p c i -> p (c i)").bitcast(I32))
        nc.sync.dma_start(out=wgs_sb[:], in_=wgs)
        nc.sync.dma_start(list2[:], offs2)
        nc.sync.dma_start(list3[:], offs3)
        nc.sync.dma_start(out=gain_sb[:], in_=gain.rearrange("(g p t) -> p g t", p=P, t=PACK))
        for q in range(4):
            nc.vector.tensor_copy(tab_s[32 * q:32 * q + 4, :].bitcast(I32), tab_s_in[32 * q:32 * q + 4, :])
        pages.append(held([P, T2], F32, "page1"))
        nc.gpsimd.memset(pages[1][:], 0.0)

        nc.vector.tensor_copy(v_s[:], tab_s[:].indirect(list1[:]))
        for lo in range(0, S, BANK):
            nc.vector.tensor_copy(
                v_w[:, lo:lo + BANK], tab_w[:].bitcast(U32).indirect(entries(list1, lo, lo + BANK))
            )

        def round_weight(copy, rounded, raw, places=slice(0, PACK)):
            copy(
                rounded.rearrange("p (t q j) -> p q j t", t=PACK, j=PACK)[:, :, :, places],
                raw[:].rearrange("p j (q t) -> p q j t", t=PACK)[:, :, :, places],
            )

        def quantise(codes, scales, rounded, lo, hi):
            nc.vector.quantize_mx(
                out=codes[:, lo:hi].bitcast(FP8X4), scales=scales[:, lo:hi], in_=rounded[:, PACK * lo:PACK * hi]
            )

        def deal(dealt, raw):
            nc.vector.tensor_copy(
                dealt.rearrange("p (g t q) -> p g q t", t=PACK, q=P), raw.rearrange("p (g q t) -> p g q t", t=PACK, q=P)
            )

        w_bf = x[1][:].rearrange("p t m -> p (t m)").bitcast(BF16)
        w31_bf = [w_bf[:, 2 * g * GROUP * PACK:2 * (g + 1) * GROUP * PACK] for g in range(GROUPS)]
        w3_part, w1_part = slice(0, GROUP * PACK), slice(GROUP * PACK, 2 * GROUP * PACK)
        round_weight(nc.scalar.copy, w31_bf[0][:, w3_part], w3_raw)
        quantise(w31_c[0], w31_s[0], w31_bf[0], 0, GROUP)
        round_weight(nc.vector.tensor_copy, w31_bf[0][:, w1_part], w1_raw, slice(0, 1))
        quantise(w31_c[0], w31_s[0], w31_bf[0], GROUP, GROUP + P)
        round_weight(nc.vector.tensor_copy, w31_bf[0][:, w1_part], w1_raw, slice(1, PACK))
        deal(w2_s[:], w2_s_raw[:])
        deal(w2_c[:], w2_raw[:])
        quantise(w31_c[0], w31_s[0], w31_bf[0], GROUP + P, 2 * GROUP)

        def product(codes, scales, col, lo, spare=False):
            acc = bank(spare)
            nc.tensor.matmul_mx(
                out=acc[:], lhsT=codes[:, col:col + P].bitcast(FP8X4), lhsT_scale=scales[:, col:col + P],
                rhs=v_w[:, lo:lo + BANK].bitcast(FP8X4), rhs_scale=v_s[:, lo:lo + BANK], start=True, stop=True,
            )
            return acc

        def cosine(s):
            cos = ring.tile([P, S], F32, name="cos", bufs=3)
            for lo in range(0, S, BANK):
                y3 = product(w31_c[s // PACK], w31_s[s // PACK], s % PACK * P, lo)
                nc.scalar.activation(cos[:, lo:lo + BANK], y3[:], ACT.Abs, bias=zero[:])
            nc.scalar.activation(cos[:], cos[:], ACT.Sin, scale=-1.0, bias=math.pi / 2)
            return cos

        def tanh_half(tanh, s, lo):
            y1 = product(w31_c[s // PACK], w31_s[s // PACK], GROUP + s % PACK * P, lo)
            nc.scalar.activation(tanh[:, lo:lo + BANK], y1[:], ACT.Tanh, bias=zero[:])

        def sum_on_vector(out, tanh, s):
            for lo in range(0, S, BANK):
                tanh_half(tanh, s, lo)
                y2 = product(w2_c, w2_s, s * P, lo, spare=True)
                nc.vector.tensor_tensor(out[:, lo:lo + BANK], y2[:], tanh[:, lo:lo + BANK], ALU.add)

        def features(s, h):
            cos = cosine(s)
            if s == 0:
                tanh = ring.tile([P, S], F32, name="tanh")
                nc.vector.tensor_tensor(cos_w[:], cos[:], wgs_sb[:], ALU.mult)
                sum_on_vector(amp, tanh, s)
                nc.vector.tensor_tensor(h[:], amp[:], cos_w[:], ALU.mult)
                spent = cos
            elif s in VECTOR_SUMS:
                nc.gpsimd.tensor_tensor(cos_w[:], cos[:], wgs_sb[:], ALU.mult)
                nc.gpsimd.tensor_tensor(h[:], amp_early[:], cos_w[:], ALU.mult)
                spent = cos
            else:
                tanh = ring.tile([P, S], F32, name="tanh")
                y2_sb = ring.tile([P, S], F32, name="y2_sb")
                for lo in range(0, S, BANK):
                    tanh_half(tanh, s, lo)
                    nc.scalar.copy(y2_sb[:, lo:lo + BANK], product(w2_c, w2_s, s * P, lo)[:])
                nc.gpsimd.tensor_tensor(cos_w[:], cos[:], wgs_sb[:], ALU.mult)
                nc.gpsimd.tensor_tensor(amp[:], tanh[:], y2_sb[:], ALU.add)
                nc.gpsimd.tensor_tensor(h[:], amp[:], cos_w[:], ALU.mult)
                spent = y2_sb
            nc.vector.tensor_copy(pages[s % PAGES][:].indirect(list2[:]), h[:])
            return spent

        def read_slots(s, lo, hi):
            nc.vector.tensor_copy(x_slice(s)[:, lo:hi], pages[s % PAGES][:].indirect(entries(list3, lo, hi)))

        z_slices = {}

        def load_jam(s):
            g, t = divmod(s, PACK)
            if t == 0:
                z_slices[g] = held([P, PACK, M], BF16, "z_slices")
            rows = ring.tile([P, M], F32, name="jam_sb", bufs=4)
            nc.sync.dma_start(
                out=rows[:], in_=jam[g * GROUP:(g + 1) * GROUP, :].rearrange("(p t) m -> p t m", t=PACK)[:, t, :]
            )
            return rows

        def join_jam(s, gain_x):
            g, t = divmod(s, PACK)
            rows = load_jam(s)
            nc.scalar.activation(gain_x, x_slice(s), ACT.Copy, scale=gain_sb[:, g, t:t + 1])
            nc.gpsimd.tensor_tensor(z_slices[g][:, t, :], gain_x, rows[:], ALU.add)

        def weave(copy, woven, slices):
            copy(
                woven.rearrange("p (c i t) -> p c t i", i=4, t=PACK), slices.rearrange("p t (c i) -> p c t i", i=4)
            )

        for s in range(SLICES):
            if s == LAST:
                h = held([P, S], F32, "h", "late")
            else:
                h = ring.tile([P, S], F32, name="h")
            spent = features(s, h)
            if s == 1:
                round_weight(nc.scalar.copy, w31_bf[1][:, w3_part], w3_raw)
                round_weight(nc.scalar.copy, w31_bf[1][:, w1_part], w1_raw)
                quantise(w31_c[1], w31_s[1], w31_bf[1], 0, 2 * GROUP)
            if s + 2 in VECTOR_SUMS:
                sum_on_vector(amp_early, x_slice(s), s + 2)
            if s < LAST:
                read_slots(s, 0, M)
            if s >= JAM_LAG:
                join_jam(s - JAM_LAG, spent[:])
            if s == 0:
                w3_raw = load_weight(w3, 1)
                w1_raw = load_weight(w1, 1)
                nc.sync.dma_start(
                    out=w4_raw[:].bitcast(I32), in_=w4_words.rearrange("a p c -> p a c").bitcast(I32)
                )
                for q in range(4):
                    nc.sync.dma_start(
                        out=w4_s_raw[32 * q:32 * q + 4 * GROUPS, :].bitcast(I32),
                        in_=w4_scales[:, 4 * q:4 * q + 4, :].bitcast(I32),
                    )
            if s == PACK - 1 + JAM_LAG:
                z0_bf = held([P, M * PACK], BF16, "z0_bf", "tab_w")
                for lo in range(0, M, CHUNK):
                    weave(nc.scalar.copy, z0_bf[:, PACK * lo:PACK * (lo + CHUNK)], z_slices[0][:, :, lo:lo + CHUNK])

        join_jam(LAST - 2, cos_w[:])
        join_jam(LAST - 1, amp[:])

        late = held([P, 2 * GROUPS * H + 5 * M + H], U8, "late")
        w4_c = [late[:, 2 * a * H:2 * (a + 1) * H] for a in range(GROUPS)]
        z_c = [late[:, 4 * H:4 * H + 4 * M].bitcast(I32), held([P, M], I32, "z_c1")]
        z_s = [late[:, 4 * H + 4 * M:4 * H + 5 * M], held([P, M], U8, "z_s1")]
        w4_s = [late[:, 4 * H + 5 * M:5 * H + 5 * M], held([P, H], U8, "w4_s1")]
        rows = load_jam(LAST)
        read_slots(LAST, 0, M)
        deal(w4_s[0], w4_s_raw[:])
        for q in range(4):
            nc.sync.dma_start(
                out=w4_s[1][32 * q:32 * q + 4, :].bitcast(I32), in_=w4_s[0][32 * q + 4:32 * q + 8, :].bitcast(I32)
            )
        deal(w4_c[0].bitcast(U16), w4_raw[:, 0, :].bitcast(U16))
        quantise(z_c[0], z_s[0], z0_bf, 0, M // 2)
        for lo in range(0, M, CHUNK):
            nc.vector.scalar_tensor_tensor(
                out=z_slices[1][:, PACK - 1, lo:lo + CHUNK], in0=x_slice(LAST)[:, lo:lo + CHUNK],
                scalar=gain_sb[:, GROUPS - 1, PACK - 1:PACK], in1=rows[:, lo:lo + CHUNK], op0=ALU.mult, op1=ALU.add,
            )
        deal(w4_c[1].bitcast(U16), w4_raw[:, 1, :].bitcast(U16))
        for lo in range(0, M, CHUNK):
            z_bf = ring.tile([P, CHUNK * PACK], BF16, name="z_bf", bufs=CHUNKS, align_bytes=64)
            weave(nc.scalar.copy, z_bf[:], z_slices[1][:, :, lo:lo + CHUNK])
            nc.vector.quantize_mx(
                out=z_c[1][:, lo:lo + CHUNK].bitcast(FP8X4), scales=z_s[1][:, lo:lo + CHUNK], in_=z_bf[:]
            )
            if lo == 0:
                quantise(z_c[0], z_s[0], z0_bf, M // 2, M)

        for lo in range(0, M, CHUNK):
            cols = slice(lo, lo + CHUNK)
            passes = (0, 1) if lo == 0 else (1, 0)
            for g in range(GROUPS):
                if g == 0:
                    y = ring.tile([P, PACK, CHUNK], F32, name="y", tag="cos", bufs=3)
                else:
                    y = ring.tile([P, PACK, CHUNK], F32, name="y", tag="jam_sb", bufs=4)
                for pair in range(2):
                    acc = bank(spare=(g == 1 and pair == 1))
                    for a in passes:
                        for e in range(2):
                            col = g * GROUP + (2 * pair + e) * P
                            nc.tensor.matmul_mx(
                                out=acc[:, e * CHUNK:(e + 1) * CHUNK],
                                lhsT=w4_c[a][:, 2 * col:2 * (col + P)].bitcast(FP4X4),
                                lhsT_scale=w4_s[a][:, col:col + P],
                                rhs=z_c[a][:, cols].bitcast(FP8X4), rhs_scale=z_s[a][:, cols],
                                start=(a == passes[0] and e == 0), stop=(a == passes[1] and e == 1),
                            )
                    nc.vector.tensor_tensor(
                        y[:, 2 * pair:2 * pair + 2, :], acc[:].rearrange("p (e m) -> p e m", e=2),
                        x[g][:, 2 * pair:2 * pair + 2, cols], ALU.add,
                    )
                nc.sync.dma_start(
                    out=out_0[g * GROUP:(g + 1) * GROUP, cols].rearrange("(p t) m -> p t m", t=PACK), in_=y[:]
                )
                y_bf = ring.tile([P, CHUNK * PACK], BF16, name="y_bf", bufs=3, align_bytes=64)
                very_last = lo + CHUNK == M and g == GROUPS - 1
                weave(nc.vector.tensor_copy if very_last else nc.scalar.copy, y_bf[:], y[:])
                y_c = ring.tile([P, CHUNK], I32, name="y_c", bufs=4, align_bytes=64)
                nc.vector.quantize_mx(out=y_c[:].bitcast(FP8X4), scales=y_s[:, g, cols], in_=y_bf[:])
                nc.sync.dma_start(out=out_1[g, :, cols, :].rearrange("p m t -> p (m t)").bitcast(I32), in_=y_c[:])
        for q in range(4):
            nc.scalar.dma_start(
                out=out_2[:, 4 * q:4 * q + 4, :].rearrange("g r m -> r g m").bitcast(I32),
                in_=y_s[32 * q:32 * q + 4, :, :].bitcast(I32),
            )
